import numpy as np
import ml_dtypes


def mxq(x, axis, fmt="e4m3"):
    dtype, down = {"e4m3": (ml_dtypes.float8_e4m3fn, 7), "e5m2": (ml_dtypes.float8_e5m2, 14)}[fmt]
    v = np.moveaxis(np.asarray(x, np.float32).astype(ml_dtypes.bfloat16).astype(np.float64), axis, -1)
    blocks = v.reshape(v.shape[:-1] + (-1, 32))
    amax = np.abs(blocks).max(-1, keepdims=True)
    byte = np.maximum(np.where(amax > 0, np.frexp(amax)[1] - 1 + 127, 0) - down, 1)
    scale = np.exp2(byte - 127.0)
    codes = (blocks / scale).astype(np.float32).astype(dtype).astype(np.float64)
    return np.moveaxis((codes * scale).reshape(v.shape), -1, axis)


WIDE = False


def mx_kscale(k):
    if not WIDE:
        return np.ones(k)
    levels = np.array([10, -10, 5, -5, 0])
    if k % 512:
        return np.exp2(np.random.permutation(np.resize(levels, k // 32))).repeat(32)
    a = np.empty((k // 512, 16))
    for p in range(k // 512):
        a[p, :8] = np.random.permutation(np.resize(levels, 8))
        for g in range(8):
            far = levels[np.abs(levels - a[p, g]) >= 10]
            a[p, g + 8] = far[np.random.randint(len(far))]
    return np.exp2(a.ravel()).repeat(32)


def f64(x):
    return np.asarray(x).astype(np.float64)


def striped(idx):
    return np.tile(idx.reshape(-1, 16).T, (8, 1)).astype(np.uint16)


def unstriped(offs):
    return offs[:16].T.reshape(-1).astype(np.int64)


def striped8(idx):
    return np.concatenate([x.reshape(-1, 16).T for x in idx]).astype(np.uint16)


def runs(offs, k):
    lists = np.stack([offs[16 * r : 16 * r + 16].T.reshape(-1) for r in range(8)]).astype(np.int64)
    return lists[np.arange(k) % 512 // 64]


def pack_weight(w):
    k, n = w.shape
    w = f64(np.asarray(w, np.float32).astype(ml_dtypes.bfloat16)).reshape(k // 32, 32, n)
    amax = np.abs(w).max(1)
    byte = np.clip(np.where(amax > 0, np.frexp(amax)[1] - 1 + 127 - 7, 1), 1, 254)
    scaled = (w * np.exp2(127.0 - byte)[:, None, :]).reshape(k, n).astype(np.float32)
    words = np.ascontiguousarray(scaled.reshape(k // 512, 128, 4, n).transpose(0, 1, 3, 2)).astype(ml_dtypes.float8_e4m3fn).view(np.uint8)
    return words, np.ascontiguousarray(byte.astype(np.uint8).reshape(k // 512, 16, n))


def unpack_weight(words, scales):
    g, p, n, _ = words.shape
    vals = np.ascontiguousarray(words).view(ml_dtypes.float8_e4m3fn).astype(np.float64) * np.repeat(np.exp2(scales.astype(np.float64) - 127.0), 8, axis=1)[..., None]
    return vals.transpose(0, 1, 3, 2).reshape(g * 512, n)


def gelu(v):
    return 0.5 * v * (1.0 + np.tanh(np.sqrt(2.0 / np.pi) * (v + 0.044715 * v**3)))

def planes(y):
    n, m = y.shape
    v = y.astype(np.float32).astype(ml_dtypes.bfloat16).astype(np.float64).reshape(n // 32, 32, m)
    top = np.abs(v).max(1)
    byte = np.clip(np.where(top > 0, np.frexp(top)[1] - 1 + 127 - 7, 1), 1, 254)
    codes = (v * np.exp2(127.0 - byte)[:, None, :]).reshape(n, m).astype(np.float32).astype(ml_dtypes.float8_e4m3fn).view(np.uint8)
    words = codes.reshape(n // 512, 128, 4, m).transpose(0, 1, 3, 2)
    return np.ascontiguousarray(words), np.ascontiguousarray(byte.astype(np.uint8).reshape(n // 512, 16, m))


K, T, S, N, U, H = 512, 2048, 512, 512, 1024, 512


def setup_inputs():
    n = np.random.standard_normal
    s = mx_kscale(K)[:, None]
    u = mx_kscale(S)
    packed_xT = pack_weight(n((K, T)) * s)
    packed_w1 = pack_weight(n((S, N)) / np.sqrt(S) / u[:, None])
    return {
        "x_words": packed_xT[0],
        "x_scales": packed_xT[1],
        "wa": (n((K, H)) / np.sqrt(K) / s).astype(np.float32),
        "gt": (np.random.uniform(0.5, 1.5, (S, 1)) * u[:, None]).astype(np.float32),
        "w1_words": packed_w1[0],
        "w1_scales": packed_w1[1],
        "offs": striped(np.random.permutation(T)[:S]),
        "fl": striped8(np.stack([np.random.permutation(U)[:H] for _ in range(8)])),
    }


def reference(x_words, x_scales, wa, gt, w1_words, w1_scales, offs, fl):
    xq = unpack_weight(x_words, x_scales)[:, unstriped(offs)]
    y = xq.T @ mxq(f64(wa), 0, "e4m3")
    e = f64(gt) * gelu(y)
    z = np.zeros((S, U))
    z[np.arange(S)[:, None], runs(fl, S)] = e
    out_0 = unpack_weight(w1_words, w1_scales).T @ mxq(z, 0, "e4m3")
    return (out_0,) + planes(out_0)

@@ -1,0 +1,214 @@
+from contextlib import ExitStack
+
+import concourse.mybir as mybir
+
+K, T, S, H, U, N = 512, 2048, 512, 512, 1024, 512
+FLOPS = 2 * K * S * H + 2 * S * N * U
+
+F32 = mybir.dt.float32
+BF16 = mybir.dt.bfloat16
+I32 = mybir.dt.int32
+U32 = mybir.dt.uint32
+U16 = mybir.dt.uint16
+U8 = mybir.dt.uint8
+FP8X4 = mybir.dt.float8_e4m3fn_x4
+GELU = mybir.ActivationFunctionType.Gelu_apprx_tanh
+COPY = mybir.ActivationFunctionType.Copy
+MULT = mybir.AluOpType.mult
+
+P = 128
+PACK = 4
+QUADS = 4
+PIECE = 128
+PIECES = H // PIECE
+CHUNKS = ((0, 128), (128, 384), (384, 640), (640, 896), (896, 1024))
+THIRD_ROW_SPANS = ((0, 384), (384, 896), (896, 1024))
+BANK = 512
+
+
+def load_scale_rows(queues, plane, rows):
+    for q in range(QUADS):
+        queues[q % len(queues)].dma_start(out=plane[32 * q : 32 * q + 4, :].bitcast(I32), in_=rows[4 * q : 4 * q + 4, :].bitcast(I32))
+
+
+def deal(nc, dealt, plain):
+    nc.vector.tensor_copy(out=dealt.rearrange("p (t m) -> p m t", t=PACK), in_=plain.rearrange("p (m t) -> p m t", t=PACK))
+
+
+def interleave_views(packed, rows):
+    return packed.rearrange("p (c i) t -> p c t i", i=4), rows.rearrange("p t (c i) -> p c t i", i=4)
+
+
+def tile_picked_blkmix_gelu_po_kernel(
+    tc, x_words, x_scales, wa, gt, w1_words, w1_scales, offs, fl, out_0, out_1, out_2
+):
+    nc = tc.nc
+    with ExitStack() as ctx:
+        sb = ctx.enter_context(tc.tile_pool(name="sb", bufs=1))
+        ps = ctx.enter_context(tc.psum_pool(name="ps", bufs=1))
+
+        offs_sb = sb.tile([P, S // 16], U16, name="offs_sb")
+        fl_sb = sb.tile([P, H // 16], U16, name="fl_sb")
+        xw_all = sb.tile([P, T], I32, name="xw_all", align_bytes=64)
+        xs_all = sb.tile([P, T], U8, name="xs_all", align_bytes=64)
+        w1w_raw = sb.tile([P, N], I32, name="w1w_raw", align_bytes=64)
+        w1s_raw = sb.tile([P, N], U8, name="w1s_raw", align_bytes=64)
+        gt_sb = sb.tile([P, PACK], F32, name="gt_sb")
+        wa_raw = [sb.tile([P, PACK, PIECE], F32, name="wa_raw%d" % n, tag="piece%d" % n, align_bytes=64) for n in range(PIECES)]
+        z32 = [sb.tile([P, U], F32, name="z32_%d" % t, align_bytes=64) for t in range(PACK)]
+
+        nc.vector.memset(xs_all[:].bitcast(I32), 0)
+        nc.vector.memset(w1s_raw[:].bitcast(I32), 0)
+        nc.sync.dma_start(offs_sb[:], offs)
+        nc.sync.dma_start(fl_sb[:], fl)
+        load_scale_rows((nc.scalar, nc.sync), xs_all, x_scales[0])
+        nc.sync.dma_start(out=xw_all[:], in_=x_words[0].rearrange("p n t -> p (n t)").bitcast(I32))
+        wa_rows = wa.rearrange("(p j) c -> p j c", j=PACK)
+        for n in range(PIECES):
+            nc.sync.dma_start(out=wa_raw[n][:], in_=wa_rows[:, :, PIECE * n : PIECE * (n + 1)])
+        nc.sync.dma_start(out=w1w_raw[:], in_=w1_words[0].rearrange("p n t -> p (n t)").bitcast(I32))
+        nc.sync.dma_start(out=gt_sb[:], in_=gt.rearrange("(p t) o -> p (t o)", t=PACK))
+        load_scale_rows((nc.sync,), w1s_raw, w1_scales[0])
+        for t in range(PACK):
+            nc.vector.memset(z32[t][:].bitcast(I32), 0)
+
+        warm = sb.tile([P, 1], F32, name="warm")
+        nc.scalar.activation(out=warm[:], in_=z32[0][:, 0:1], func=GELU)
+
+        xs_picked = sb.tile([P, S], U8, name="xs_picked", align_bytes=64)
+        xs = sb.tile([P, S], U8, name="xs", align_bytes=64)
+        xw_picked = sb.tile([P, S], U32, name="xw_picked", align_bytes=64)
+        xw = sb.tile([P, S], U32, name="xw", tag="xw_then_z", align_bytes=64)
+        nc.vector.tensor_copy(out=xs_picked[:], in_=xs_all[:].indirect(offs_sb[:]))
+        deal(nc, xs[:], xs_picked[:])
+        nc.vector.tensor_copy(out=xw_picked[:], in_=xw_all[:].bitcast(U32).indirect(offs_sb[:]))
+        deal(nc, xw[:], xw_picked[:])
+
+        wa_w = sb.tile([P, H], U32, name="wa_w", align_bytes=64)
+        wa_s = sb.tile([P, H], U8, name="wa_s", align_bytes=64)
+
+        def project(t, a, b, bank, tag):
+            y = ps.tile([P, BANK], F32, name="y", tag="bank%d" % bank)
+            tok = slice(P * t, P * (t + 1))
+            nc.tensor.matmul_mx(
+                out=y[:, 0 : b - a],
+                lhsT=xw[:, tok].bitcast(FP8X4),
+                lhsT_scale=xs[:, tok],
+                rhs=wa_w[:, a:b].bitcast(FP8X4),
+                rhs_scale=wa_s[:, a:b],
+                start=True,
+                stop=True,
+            )
+            g = sb.tile([P, b - a], F32, name="g", tag=tag, align_bytes=64)
+            nc.scalar.activation(out=g[:], in_=y[:, 0 : b - a], func=GELU)
+            return g
+
+        def scatter(t, a, b, g):
+            nc.vector.tensor_copy(out=z32[t][:].indirect(fl_sb[:, a // 16 : b // 16]), in_=g[:])
+
+        def quantise_wa(n):
+            wa_bf = sb.tile([P, PIECE, PACK], BF16, name="wa_bf%d" % n, align_bytes=64)
+            dst, src = interleave_views(wa_bf[:], wa_raw[n][:])
+            nc.scalar.copy(out=dst, in_=src)
+            piece = slice(PIECE * n, PIECE * (n + 1))
+            nc.vector.quantize_mx(
+                out=wa_w[:, piece].bitcast(FP8X4), scales=wa_s[:, piece], in_=wa_bf[:].rearrange("p c t -> p (c t)")
+            )
+
+        quantise_wa(0)
+        for n in range(PIECES):
+            if n + 1 < PIECES:
+                quantise_wa(n + 1)
+            tag = "piece%d" % (n + 1) if n + 1 < PIECES else "row0"
+            a, b = PIECE * n, PIECE * (n + 1)
+            scatter(0, a, b, project(0, a, b, n, tag))
+        g_rows = {t: project(t, 0, H, PIECES + t - 1, "row%d" % t) for t in range(1, PACK)}
+
+        w1w = sb.tile([P, N], U32, name="w1w", align_bytes=64)
+        w1s = sb.tile([P, N], U8, name="w1s", align_bytes=64)
+        deal(nc, w1w[:], w1w_raw[:].bitcast(U32))
+        deal(nc, w1s[:], w1s_raw[:])
+
+        widths = [b - a for a, b in CHUNKS]
+        cols = [slice(a, b) for a, b in CHUNKS]
+        chunks = range(len(CHUNKS))
+        z_bf = sb.tile([P, U, PACK], BF16, name="z_bf", tag="xw_then_z", align_bytes=64)
+        last = PACK - 1
+
+        for t in range(PACK):
+            if t > 0:
+                scatter(t, 0, H, g_rows[t])
+            if t < last - 1:
+                nc.scalar.activation(out=z_bf[:, :, t], in_=z32[t][:], func=COPY, scale=gt_sb[:, t : t + 1])
+            if t == last - 1:
+                for a, b in THIRD_ROW_SPANS:
+                    nc.scalar.activation(
+                        out=z_bf[:, a:b, t : t + 2],
+                        in_=z32[t][:, a:b].unsqueeze(2).to_broadcast([P, b - a, 2]),
+                        func=COPY,
+                        scale=gt_sb[:, t : t + 1],
+                    )
+
+        z_w = [sb.tile([P, widths[c]], U32, name="z_w%d" % c, align_bytes=64) for c in chunks]
+        z_s = [sb.tile([P, widths[c]], U8, name="z_s%d" % c, align_bytes=64) for c in chunks]
+
+        def weigh_on_vector(c):
+            nc.vector.tensor_scalar(
+                out=z_bf[:, cols[c], last], in0=z32[last][:, cols[c]], scalar1=gt_sb[:, last : last + 1], scalar2=None, op0=MULT
+            )
+
+        def quantise_z(c):
+            nc.vector.quantize_mx(out=z_w[c][:].bitcast(FP8X4), scales=z_s[c][:], in_=z_bf[:, cols[c], :].rearrange("p c t -> p (c t)"))
+
+        weigh_on_vector(0)
+        for c in chunks:
+            if c + 1 < len(CHUNKS):
+                weigh_on_vector(c + 1)
+            quantise_z(c)
+
+        out_rows = out_0.rearrange("(p t) n -> p t n", t=PACK)
+        out_words = out_1[0].rearrange("p n t -> p (n t)").bitcast(I32)
+        o_s = sb.tile([P, U], U8, name="o_s", align_bytes=64)
+        o32 = [sb.tile([P, PACK, widths[c]], F32, name="o32_%d" % c, align_bytes=64) for c in chunks]
+        o_bf = [sb.tile([P, widths[c], PACK], BF16, name="o_bf%d" % c, align_bytes=64) for c in chunks]
+        o_w = [sb.tile([P, widths[c]], I32, name="o_w%d" % c, align_bytes=64) for c in chunks]
+
+        def mix(c, bank):
+            per_bank = BANK // widths[c]
+            for t0 in range(0, PACK, per_bank):
+                acc = ps.tile([P, per_bank, widths[c]], F32, name="acc", tag="bank%d" % (bank % 8))
+                bank = bank + 1
+                for u in range(per_bank):
+                    rows = slice(P * (t0 + u), P * (t0 + u + 1))
+                    nc.tensor.matmul_mx(
+                        out=acc[:, u, :],
+                        lhsT=w1w[:, rows].bitcast(FP8X4),
+                        lhsT_scale=w1s[:, rows],
+                        rhs=z_w[c][:].bitcast(FP8X4),
+                        rhs_scale=z_s[c][:],
+                        start=True,
+                        stop=True,
+                    )
+                nc.scalar.copy(out=o32[c][:, t0 : t0 + per_bank, :], in_=acc[:])
+                nc.sync.dma_start(out=out_rows[:, t0 : t0 + per_bank, cols[c]], in_=o32[c][:, t0 : t0 + per_bank, :])
+            return bank
+
+        def round_out(c):
+            dst, src = interleave_views(o_bf[c][:], o32[c][:])
+            nc.vector.tensor_copy(out=dst, in_=src)
+
+        def quantise_out(c):
+            nc.vector.quantize_mx(
+                out=o_w[c][:].bitcast(FP8X4), scales=o_s[:, cols[c]], in_=o_bf[c][:].rearrange("p c t -> p (c t)")
+            )
+            nc.sync.dma_start(out=out_words[:, cols[c]], in_=o_w[c][:])
+
+        bank = 7
+        for c in chunks:
+            bank = mix(c, bank)
+        for c in chunks:
+            round_out(c)
+            quantise_out(c)
+        for q in range(QUADS):
+            queue = nc.scalar if q % 2 else nc.sync
+            queue.dma_start(out=out_2[0, 4 * q : 4 * q + 4, :].bitcast(I32), in_=o_s[32 * q : 32 * q + 4, :].bitcast(I32))

@@ -22,7 +22,9 @@ QUADS = 4
 PIECE = 128
 PIECES = H // PIECE
 CHUNKS = ((0, 128), (128, 384), (384, 640), (640, 896), (896, 1024))
-THIRD_ROW_SPANS = ((0, 384), (384, 896), (896, 1024))
+SPLIT = 768
+ROUNDS = ((0, 2), (2, 3), (3, 4), (4, 5))
+THIRD_ROW_SPANS = ((0, 384), (384, SPLIT))
 BANK = 512
 
 
@@ -57,23 +59,30 @@ def tile_picked_blkmix_gelu_po_kernel(
         wa_raw = [sb.tile([P, PACK, PIECE], F32, name="wa_raw%d" % n, tag="piece%d" % n, align_bytes=64) for n in range(PIECES)]
         z32 = [sb.tile([P, U], F32, name="z32_%d" % t, align_bytes=64) for t in range(PACK)]
 
-        nc.vector.memset(xs_all[:].bitcast(I32), 0)
-        nc.vector.memset(w1s_raw[:].bitcast(I32), 0)
+        nc.gpsimd.memset(xs_all[:].bitcast(I32), 0)
         nc.sync.dma_start(offs_sb[:], offs)
         nc.sync.dma_start(fl_sb[:], fl)
         load_scale_rows((nc.scalar, nc.sync), xs_all, x_scales[0])
         nc.sync.dma_start(out=xw_all[:], in_=x_words[0].rearrange("p n t -> p (n t)").bitcast(I32))
         wa_rows = wa.rearrange("(p j) c -> p j c", j=PACK)
-        for n in range(PIECES):
+
+        def load_wa(n):
             nc.sync.dma_start(out=wa_raw[n][:], in_=wa_rows[:, :, PIECE * n : PIECE * (n + 1)])
+
+        load_wa(0)
+        load_wa(1)
         nc.sync.dma_start(out=w1w_raw[:], in_=w1_words[0].rearrange("p n t -> p (n t)").bitcast(I32))
+        load_wa(2)
+        load_wa(3)
         nc.sync.dma_start(out=gt_sb[:], in_=gt.rearrange("(p t) o -> p (t o)", t=PACK))
+        nc.gpsimd.memset(w1s_raw[:].bitcast(I32), 0)
         load_scale_rows((nc.sync,), w1s_raw, w1_scales[0])
         for t in range(PACK):
-            nc.vector.memset(z32[t][:].bitcast(I32), 0)
+            engine = nc.vector if t == PACK - 1 else nc.gpsimd
+            engine.memset(z32[t][:], 0.0)
 
         warm = sb.tile([P, 1], F32, name="warm")
-        nc.scalar.activation(out=warm[:], in_=z32[0][:, 0:1], func=GELU)
+        nc.scalar.activation(out=warm[:], in_=z32[PACK - 1][:, 0:1], func=GELU)
 
         xs_picked = sb.tile([P, S], U8, name="xs_picked", align_bytes=64)
         xs = sb.tile([P, S], U8, name="xs", align_bytes=64)
@@ -148,13 +157,16 @@ def tile_picked_blkmix_gelu_po_kernel(
                         func=COPY,
                         scale=gt_sb[:, t : t + 1],
                     )
+            if t >= last - 1:
+                nc.scalar.activation(out=z_bf[:, SPLIT:U, t], in_=z32[t][:, SPLIT:U], func=COPY, scale=gt_sb[:, t : t + 1])
 
         z_w = [sb.tile([P, widths[c]], U32, name="z_w%d" % c, align_bytes=64) for c in chunks]
         z_s = [sb.tile([P, widths[c]], U8, name="z_s%d" % c, align_bytes=64) for c in chunks]
 
         def weigh_on_vector(c):
+            mine = slice(cols[c].start, min(cols[c].stop, SPLIT))
             nc.vector.tensor_scalar(
-                out=z_bf[:, cols[c], last], in0=z32[last][:, cols[c]], scalar1=gt_sb[:, last : last + 1], scalar2=None, op0=MULT
+                out=z_bf[:, mine, last], in0=z32[last][:, mine], scalar1=gt_sb[:, last : last + 1], scalar2=None, op0=MULT
             )
 
         def quantise_z(c):
@@ -162,18 +174,20 @@ def tile_picked_blkmix_gelu_po_kernel(
 
         weigh_on_vector(0)
         for c in chunks:
-            if c + 1 < len(CHUNKS):
+            if c + 1 < len(CHUNKS) and CHUNKS[c + 1][0] < SPLIT:
                 weigh_on_vector(c + 1)
             quantise_z(c)
 
         out_rows = out_0.rearrange("(p t) n -> p t n", t=PACK)
         out_words = out_1[0].rearrange("p n t -> p (n t)").bitcast(I32)
         o_s = sb.tile([P, U], U8, name="o_s", align_bytes=64)
-        o32 = [sb.tile([P, PACK, widths[c]], F32, name="o32_%d" % c, align_bytes=64) for c in chunks]
-        o_bf = [sb.tile([P, widths[c], PACK], BF16, name="o_bf%d" % c, align_bytes=64) for c in chunks]
-        o_w = [sb.tile([P, widths[c]], I32, name="o_w%d" % c, align_bytes=64) for c in chunks]
+        o_w = sb.tile([P, U], I32, name="o_w", align_bytes=64)
+        o_bf = sb.tile([P, U, PACK], BF16, name="o_bf", align_bytes=64)
+        spans = [slice(CHUNKS[lo][0], CHUNKS[hi - 1][1]) for lo, hi in ROUNDS]
+        o32 = [sb.tile([P, PACK, s.stop - s.start], F32, name="o32_%d" % s.start, align_bytes=64) for s in spans]
 
-        def mix(c, bank):
+        def mix(r, c, bank):
+            here = slice(cols[c].start - spans[r].start, cols[c].stop - spans[r].start)
             per_bank = BANK // widths[c]
             for t0 in range(0, PACK, per_bank):
                 acc = ps.tile([P, per_bank, widths[c]], F32, name="acc", tag="bank%d" % (bank % 8))
@@ -189,26 +203,27 @@ def tile_picked_blkmix_gelu_po_kernel(
                         start=True,
                         stop=True,
                     )
-                nc.scalar.copy(out=o32[c][:, t0 : t0 + per_bank, :], in_=acc[:])
-                nc.sync.dma_start(out=out_rows[:, t0 : t0 + per_bank, cols[c]], in_=o32[c][:, t0 : t0 + per_bank, :])
+                nc.scalar.copy(out=o32[r][:, t0 : t0 + per_bank, here], in_=acc[:])
+                nc.sync.dma_start(out=out_rows[:, t0 : t0 + per_bank, cols[c]], in_=o32[r][:, t0 : t0 + per_bank, here])
+                if c == len(CHUNKS) - 1:
+                    nc.scalar.copy(out=o_bf[:, cols[c], :], in_=acc[:].rearrange("p t n -> p n t"))
             return bank
 
-        def round_out(c):
-            dst, src = interleave_views(o_bf[c][:], o32[c][:])
-            nc.vector.tensor_copy(out=dst, in_=src)
-
-        def quantise_out(c):
-            nc.vector.quantize_mx(
-                out=o_w[c][:].bitcast(FP8X4), scales=o_s[:, cols[c]], in_=o_bf[c][:].rearrange("p c t -> p (c t)")
-            )
-            nc.sync.dma_start(out=out_words[:, cols[c]], in_=o_w[c][:])
-
         bank = 7
-        for c in chunks:
-            bank = mix(c, bank)
-        for c in chunks:
-            round_out(c)
-            quantise_out(c)
+        for r, (lo, hi) in enumerate(ROUNDS):
+            for c in range(lo, hi):
+                bank = mix(r, c, bank)
+        for r, span in enumerate(spans):
+            if r < len(ROUNDS) - 1:
+                dst, src = interleave_views(o_bf[:, span, :], o32[r][:])
+                nc.vector.tensor_copy(out=dst, in_=src)
+            for a, b in CHUNKS:
+                if span.start <= a and b <= span.stop:
+                    nc.vector.quantize_mx(
+                        out=o_w[:, a:b].bitcast(FP8X4), scales=o_s[:, a:b], in_=o_bf[:, a:b, :].rearrange("p c t -> p (c t)")
+                    )
+        for queue, a, b in ((nc.sync, 0, 640), (nc.scalar, 640, 896), (nc.sync, 896, U)):
+            queue.dma_start(out=out_words[:, a:b], in_=o_w[:, a:b])
         for q in range(QUADS):
             queue = nc.scalar if q % 2 else nc.sync
             queue.dma_start(out=out_2[0, 4 * q : 4 * q + 4, :].bitcast(I32), in_=o_s[32 * q : 32 * q + 4, :].bitcast(I32))

@@ -22,9 +22,8 @@ QUADS = 4
 PIECE = 128
 PIECES = H // PIECE
 CHUNKS = ((0, 128), (128, 384), (384, 640), (640, 896), (896, 1024))
-SPLIT = 768
+THIRD_ROW_SPANS = ((0, 384), (384, 896), (896, 1024))
 ROUNDS = ((0, 2), (2, 3), (3, 4), (4, 5))
-THIRD_ROW_SPANS = ((0, 384), (384, SPLIT))
 BANK = 512
 
 
@@ -35,6 +34,10 @@ def load_scale_rows(queues, plane, rows):
 
 def deal(nc, dealt, plain):
     nc.vector.tensor_copy(out=dealt.rearrange("p (t m) -> p m t", t=PACK), in_=plain.rearrange("p (m t) -> p m t", t=PACK))
+
+
+def deal_on_gpsimd(nc, dealt, plain):
+    nc.gpsimd.tensor_copy(out=dealt.rearrange("p (t m) -> p t m", t=PACK), in_=plain.rearrange("p (m t) -> p t m", t=PACK))
 
 
 def interleave_views(packed, rows):
@@ -69,20 +72,18 @@ def tile_picked_blkmix_gelu_po_kernel(
         def load_wa(n):
             nc.sync.dma_start(out=wa_raw[n][:], in_=wa_rows[:, :, PIECE * n : PIECE * (n + 1)])
 
-        load_wa(0)
-        load_wa(1)
+        for n in range(PIECES):
+            load_wa(n)
         nc.sync.dma_start(out=w1w_raw[:], in_=w1_words[0].rearrange("p n t -> p (n t)").bitcast(I32))
-        load_wa(2)
-        load_wa(3)
         nc.sync.dma_start(out=gt_sb[:], in_=gt.rearrange("(p t) o -> p (t o)", t=PACK))
+        for t in range(PACK):
+            engine = nc.vector if t >= 2 else nc.gpsimd
+            engine.memset(z32[t][:], 0.0)
         nc.gpsimd.memset(w1s_raw[:].bitcast(I32), 0)
         load_scale_rows((nc.sync,), w1s_raw, w1_scales[0])
-        for t in range(PACK):
-            engine = nc.vector if t == PACK - 1 else nc.gpsimd
-            engine.memset(z32[t][:], 0.0)
 
         warm = sb.tile([P, 1], F32, name="warm")
-        nc.scalar.activation(out=warm[:], in_=z32[PACK - 1][:, 0:1], func=GELU)
+        nc.scalar.activation(out=warm[:], in_=z32[2][:, 0:1], func=GELU)
 
         xs_picked = sb.tile([P, S], U8, name="xs_picked", align_bytes=64)
         xs = sb.tile([P, S], U8, name="xs", align_bytes=64)
@@ -96,7 +97,7 @@ def tile_picked_blkmix_gelu_po_kernel(
         wa_w = sb.tile([P, H], U32, name="wa_w", align_bytes=64)
         wa_s = sb.tile([P, H], U8, name="wa_s", align_bytes=64)
 
-        def project(t, a, b, bank, tag):
+        def project(t, a, b, bank, g):
             y = ps.tile([P, BANK], F32, name="y", tag="bank%d" % bank)
             tok = slice(P * t, P * (t + 1))
             nc.tensor.matmul_mx(
@@ -108,9 +109,7 @@ def tile_picked_blkmix_gelu_po_kernel(
                 start=True,
                 stop=True,
             )
-            g = sb.tile([P, b - a], F32, name="g", tag=tag, align_bytes=64)
-            nc.scalar.activation(out=g[:], in_=y[:, 0 : b - a], func=GELU)
-            return g
+            nc.scalar.activation(out=g, in_=y[:, 0 : b - a], func=GELU)
 
         def scatter(t, a, b, g):
             nc.vector.tensor_copy(out=z32[t][:].indirect(fl_sb[:, a // 16 : b // 16]), in_=g[:])
@@ -124,19 +123,19 @@ def tile_picked_blkmix_gelu_po_kernel(
                 out=wa_w[:, piece].bitcast(FP8X4), scales=wa_s[:, piece], in_=wa_bf[:].rearrange("p c t -> p (c t)")
             )
 
+        g_rows = {t: sb.tile([P, H], F32, name="g%d" % t, tag="row%d" % t, align_bytes=64) for t in range(1, PACK)}
         quantise_wa(0)
         for n in range(PIECES):
             if n + 1 < PIECES:
                 quantise_wa(n + 1)
-            tag = "piece%d" % (n + 1) if n + 1 < PIECES else "row0"
+            tag = "piece%d" % (n + 1) if n + 1 < PIECES else "g0_last"
             a, b = PIECE * n, PIECE * (n + 1)
-            scatter(0, a, b, project(0, a, b, n, tag))
-        g_rows = {t: project(t, 0, H, PIECES + t - 1, "row%d" % t) for t in range(1, PACK)}
+            g = sb.tile([P, PIECE], F32, name="g0", tag=tag, align_bytes=64)
+            project(0, a, b, n, g[:])
+            scatter(0, a, b, g)
+        for t in range(1, PACK):
+            project(t, 0, H, PIECES + t - 1, g_rows[t][:])
 
-        w1w = sb.tile([P, N], U32, name="w1w", align_bytes=64)
-        w1s = sb.tile([P, N], U8, name="w1s", align_bytes=64)
-        deal(nc, w1w[:], w1w_raw[:].bitcast(U32))
-        deal(nc, w1s[:], w1s_raw[:])
 
         widths = [b - a for a, b in CHUNKS]
         cols = [slice(a, b) for a, b in CHUNKS]
@@ -144,29 +143,30 @@ def tile_picked_blkmix_gelu_po_kernel(
         z_bf = sb.tile([P, U, PACK], BF16, name="z_bf", tag="xw_then_z", align_bytes=64)
         last = PACK - 1
 
+        def weigh_on_scalar(dst, src, t):
+            nc.scalar.activation(out=dst, in_=src, func=COPY, scale=gt_sb[:, t : t + 1])
+
         for t in range(PACK):
             if t > 0:
                 scatter(t, 0, H, g_rows[t])
+            if t == 1:
+                w1w = sb.tile([P, N], U32, name="w1w", tag="row1", align_bytes=64)
+                deal_on_gpsimd(nc, w1w[:], w1w_raw[:].bitcast(U32))
+            if t == 2:
+                w1s = sb.tile([P, N], U8, name="w1s", tag="row2", align_bytes=64)
+                deal_on_gpsimd(nc, w1s[:], w1s_raw[:])
             if t < last - 1:
-                nc.scalar.activation(out=z_bf[:, :, t], in_=z32[t][:], func=COPY, scale=gt_sb[:, t : t + 1])
+                weigh_on_scalar(z_bf[:, :, t], z32[t][:], t)
             if t == last - 1:
                 for a, b in THIRD_ROW_SPANS:
-                    nc.scalar.activation(
-                        out=z_bf[:, a:b, t : t + 2],
-                        in_=z32[t][:, a:b].unsqueeze(2).to_broadcast([P, b - a, 2]),
-                        func=COPY,
-                        scale=gt_sb[:, t : t + 1],
-                    )
-            if t >= last - 1:
-                nc.scalar.activation(out=z_bf[:, SPLIT:U, t], in_=z32[t][:, SPLIT:U], func=COPY, scale=gt_sb[:, t : t + 1])
+                    weigh_on_scalar(z_bf[:, a:b, t : t + 2], z32[t][:, a:b].unsqueeze(2).to_broadcast([P, b - a, 2]), t)
 
         z_w = [sb.tile([P, widths[c]], U32, name="z_w%d" % c, align_bytes=64) for c in chunks]
         z_s = [sb.tile([P, widths[c]], U8, name="z_s%d" % c, align_bytes=64) for c in chunks]
 
         def weigh_on_vector(c):
-            mine = slice(cols[c].start, min(cols[c].stop, SPLIT))
             nc.vector.tensor_scalar(
-                out=z_bf[:, mine, last], in0=z32[last][:, mine], scalar1=gt_sb[:, last : last + 1], scalar2=None, op0=MULT
+                out=z_bf[:, cols[c], last], in0=z32[last][:, cols[c]], scalar1=gt_sb[:, last : last + 1], scalar2=None, op0=MULT
             )
 
         def quantise_z(c):
@@ -174,7 +174,7 @@ def tile_picked_blkmix_gelu_po_kernel(
 
         weigh_on_vector(0)
         for c in chunks:
-            if c + 1 < len(CHUNKS) and CHUNKS[c + 1][0] < SPLIT:
+            if c + 1 < len(CHUNKS):
                 weigh_on_vector(c + 1)
             quantise_z(c)
 
@@ -205,8 +205,6 @@ def tile_picked_blkmix_gelu_po_kernel(
                     )
                 nc.scalar.copy(out=o32[r][:, t0 : t0 + per_bank, here], in_=acc[:])
                 nc.sync.dma_start(out=out_rows[:, t0 : t0 + per_bank, cols[c]], in_=o32[r][:, t0 : t0 + per_bank, here])
-                if c == len(CHUNKS) - 1:
-                    nc.scalar.copy(out=o_bf[:, cols[c], :], in_=acc[:].rearrange("p t n -> p n t"))
             return bank
 
         bank = 7
@@ -214,15 +212,14 @@ def tile_picked_blkmix_gelu_po_kernel(
             for c in range(lo, hi):
                 bank = mix(r, c, bank)
         for r, span in enumerate(spans):
-            if r < len(ROUNDS) - 1:
-                dst, src = interleave_views(o_bf[:, span, :], o32[r][:])
-                nc.vector.tensor_copy(out=dst, in_=src)
+            dst, src = interleave_views(o_bf[:, span, :], o32[r][:])
+            nc.vector.tensor_copy(out=dst, in_=src)
             for a, b in CHUNKS:
                 if span.start <= a and b <= span.stop:
                     nc.vector.quantize_mx(
                         out=o_w[:, a:b].bitcast(FP8X4), scales=o_s[:, a:b], in_=o_bf[:, a:b, :].rearrange("p c t -> p (c t)")
                     )
-        for queue, a, b in ((nc.sync, 0, 640), (nc.scalar, 640, 896), (nc.sync, 896, U)):
+        for queue, a, b in ((nc.sync, 0, 640), (nc.sync, 640, 896), (nc.sync, 896, U)):
             queue.dma_start(out=out_words[:, a:b], in_=o_w[:, a:b])
         for q in range(QUADS):
             queue = nc.scalar if q % 2 else nc.sync

@@ -15,29 +15,31 @@ FP8X4 = mybir.dt.float8_e4m3fn_x4
 GELU = mybir.ActivationFunctionType.Gelu_apprx_tanh
 COPY = mybir.ActivationFunctionType.Copy
 MULT = mybir.AluOpType.mult
+ADD = mybir.AluOpType.add
 
 P = 128
 PACK = 4
 QUADS = 4
-PIECE = 128
-PIECES = H // PIECE
-CHUNKS = ((0, 128), (128, 384), (384, 640), (640, 896), (896, 1024))
-THIRD_ROW_SPANS = ((0, 384), (384, 896), (896, 1024))
-ROUNDS = ((0, 2), (2, 3), (3, 4), (4, 5))
 BANK = 512
+BANKS = 8
+WA_PIECES = ((0, 128), (128, 256), (256, 512))
+CHUNKS = ((0, 128), (128, 384), (384, 640), (640, 896), (896, 1024))
+SCALAR_FROM = 768
+ROUNDS = ((0, 2), (2, 3), (3, 4), (4, 5))
+WORD_STORES = ((0, 640), (640, 896), (896, 1024))
 
 
-def load_scale_rows(queues, plane, rows):
+def load_scale_rows(queue, plane, rows):
     for q in range(QUADS):
-        queues[q % len(queues)].dma_start(out=plane[32 * q : 32 * q + 4, :].bitcast(I32), in_=rows[4 * q : 4 * q + 4, :].bitcast(I32))
+        queue.dma_start(out=plane[32 * q : 32 * q + 4, :].bitcast(I32), in_=rows[4 * q : 4 * q + 4, :].bitcast(I32))
 
 
-def deal(nc, dealt, plain):
-    nc.vector.tensor_copy(out=dealt.rearrange("p (t m) -> p m t", t=PACK), in_=plain.rearrange("p (m t) -> p m t", t=PACK))
+def dealt_in_stream_order(dealt):
+    return dealt.rearrange("p (t m) -> p m t", t=PACK)
 
 
-def deal_on_gpsimd(nc, dealt, plain):
-    nc.gpsimd.tensor_copy(out=dealt.rearrange("p (t m) -> p t m", t=PACK), in_=plain.rearrange("p (m t) -> p t m", t=PACK))
+def deal(engine, dealt, plain):
+    engine.tensor_copy(out=dealt.rearrange("p (t m) -> p t m", t=PACK), in_=plain.rearrange("p (m t) -> p t m", t=PACK))
 
 
 def interleave_views(packed, rows):
@@ -59,45 +61,63 @@ def tile_picked_blkmix_gelu_po_kernel(
         w1w_raw = sb.tile([P, N], I32, name="w1w_raw", align_bytes=64)
         w1s_raw = sb.tile([P, N], U8, name="w1s_raw", align_bytes=64)
         gt_sb = sb.tile([P, PACK], F32, name="gt_sb")
-        wa_raw = [sb.tile([P, PACK, PIECE], F32, name="wa_raw%d" % n, tag="piece%d" % n, align_bytes=64) for n in range(PIECES)]
-        z32 = [sb.tile([P, U], F32, name="z32_%d" % t, align_bytes=64) for t in range(PACK)]
-
-        nc.gpsimd.memset(xs_all[:].bitcast(I32), 0)
-        nc.sync.dma_start(offs_sb[:], offs)
-        nc.sync.dma_start(fl_sb[:], fl)
-        load_scale_rows((nc.scalar, nc.sync), xs_all, x_scales[0])
-        nc.sync.dma_start(out=xw_all[:], in_=x_words[0].rearrange("p n t -> p (n t)").bitcast(I32))
+        wa_raw = [
+            sb.tile([P, PACK, b - a], F32, name="wa_raw%d" % n, tag="piece%d" % n, align_bytes=64) for n, (a, b) in enumerate(WA_PIECES)
+        ]
+        first, second, third, last = 0, 2, 1, 3
+        z32 = {}
         wa_rows = wa.rearrange("(p j) c -> p j c", j=PACK)
 
         def load_wa(n):
-            nc.sync.dma_start(out=wa_raw[n][:], in_=wa_rows[:, :, PIECE * n : PIECE * (n + 1)])
+            a, b = WA_PIECES[n]
+            nc.sync.dma_start(out=wa_raw[n][:], in_=wa_rows[:, :, a:b])
 
-        for n in range(PIECES):
-            load_wa(n)
+        nc.gpsimd.memset(xs_all[:].bitcast(I32), 0)
+        warm = sb.tile([P, 1], F32, name="warm")
+        nc.gpsimd.memset(warm[:], 0.0)
+        warmed = sb.tile([P, 1], F32, name="warmed")
+        nc.scalar.activation(out=warmed[:], in_=warm[:], func=GELU)
+        nc.sync.dma_start(offs_sb[:], offs)
+        load_wa(0)
+        load_scale_rows(nc.sync, xs_all, x_scales[0])
+        nc.sync.dma_start(out=xw_all[:], in_=x_words[0].rearrange("p n t -> p (n t)").bitcast(I32))
+        load_wa(1)
+        nc.sync.dma_start(fl_sb[:], fl)
+        load_wa(2)
         nc.sync.dma_start(out=w1w_raw[:], in_=w1_words[0].rearrange("p n t -> p (n t)").bitcast(I32))
         nc.sync.dma_start(out=gt_sb[:], in_=gt.rearrange("(p t) o -> p (t o)", t=PACK))
-        for t in range(PACK):
-            engine = nc.vector if t >= 2 else nc.gpsimd
-            engine.memset(z32[t][:], 0.0)
         nc.gpsimd.memset(w1s_raw[:].bitcast(I32), 0)
-        load_scale_rows((nc.sync,), w1s_raw, w1_scales[0])
-
-        warm = sb.tile([P, 1], F32, name="warm")
-        nc.scalar.activation(out=warm[:], in_=z32[2][:, 0:1], func=GELU)
+        load_scale_rows(nc.sync, w1s_raw, w1_scales[0])
 
         xs_picked = sb.tile([P, S], U8, name="xs_picked", align_bytes=64)
         xs = sb.tile([P, S], U8, name="xs", align_bytes=64)
-        xw_picked = sb.tile([P, S], U32, name="xw_picked", align_bytes=64)
-        xw = sb.tile([P, S], U32, name="xw", tag="xw_then_z", align_bytes=64)
-        nc.vector.tensor_copy(out=xs_picked[:], in_=xs_all[:].indirect(offs_sb[:]))
-        deal(nc, xs[:], xs_picked[:])
-        nc.vector.tensor_copy(out=xw_picked[:], in_=xw_all[:].bitcast(U32).indirect(offs_sb[:]))
-        deal(nc, xw[:], xw_picked[:])
-
+        xw = sb.tile([P, S], U32, name="xw", align_bytes=64)
         wa_w = sb.tile([P, H], U32, name="wa_w", align_bytes=64)
         wa_s = sb.tile([P, H], U8, name="wa_s", align_bytes=64)
 
-        def project(t, a, b, bank, g):
+        def quantise_wa(n):
+            a, b = WA_PIECES[n]
+            wa_bf = sb.tile([P, b - a, PACK], BF16, name="wa_bf%d" % n, tag="rounded%d" % n, align_bytes=64)
+            dst, src = interleave_views(wa_bf[:], wa_raw[n][:])
+            nc.scalar.copy(out=dst, in_=src)
+            nc.vector.quantize_mx(out=wa_w[:, a:b].bitcast(FP8X4), scales=wa_s[:, a:b], in_=wa_bf[:].rearrange("p c t -> p (c t)"))
+
+        nc.vector.tensor_copy(out=xs_picked[:], in_=xs_all[:].indirect(offs_sb[:]))
+        deal(nc.vector, xs[:], xs_picked[:])
+        quantise_wa(0)
+        nc.vector.tensor_copy(out=dealt_in_stream_order(xw[:]), in_=xw_all[:].bitcast(U32).indirect(offs_sb[:]))
+        quantise_wa(1)
+
+        def clear_window(engine, t, tag):
+            z32[t] = sb.tile([P, U], F32, name="z32_%d" % t, tag=tag, align_bytes=64)
+            engine.memset(z32[t][:], 0.0)
+
+        clear_window(nc.vector, first, "window_first")
+        clear_window(nc.vector, second, "window_second")
+        clear_window(nc.gpsimd, last, "rounded0")
+        clear_window(nc.gpsimd, third, "rounded1")
+
+        def project(t, a, b, bank, tag):
             y = ps.tile([P, BANK], F32, name="y", tag="bank%d" % bank)
             tok = slice(P * t, P * (t + 1))
             nc.tensor.matmul_mx(
@@ -109,65 +129,65 @@ def tile_picked_blkmix_gelu_po_kernel(
                 start=True,
                 stop=True,
             )
-            nc.scalar.activation(out=g, in_=y[:, 0 : b - a], func=GELU)
+            g = sb.tile([P, b - a], F32, name="g", tag=tag, align_bytes=64)
+            nc.scalar.activation(out=g[:], in_=y[:, 0 : b - a], func=GELU)
+            return g
 
         def scatter(t, a, b, g):
             nc.vector.tensor_copy(out=z32[t][:].indirect(fl_sb[:, a // 16 : b // 16]), in_=g[:])
 
-        def quantise_wa(n):
-            wa_bf = sb.tile([P, PIECE, PACK], BF16, name="wa_bf%d" % n, align_bytes=64)
-            dst, src = interleave_views(wa_bf[:], wa_raw[n][:])
-            nc.scalar.copy(out=dst, in_=src)
-            piece = slice(PIECE * n, PIECE * (n + 1))
-            nc.vector.quantize_mx(
-                out=wa_w[:, piece].bitcast(FP8X4), scales=wa_s[:, piece], in_=wa_bf[:].rearrange("p c t -> p (c t)")
-            )
+        early = ((first, 0, 128, "piece1"), (second, 0, 256, "g1"), (first, 128, 256, "g2"))
+        late = (
+            (third, 0, 256, "piece2"),
+            (first, 256, 512, "g4"),
+            (second, 256, 512, "g5"),
+            (third, 256, 512, "g6"),
+            (last, 0, 512, "g7"),
+        )
+        for n, (t, a, b, tag) in enumerate(early):
+            scatter(t, a, b, project(t, a, b, n, tag))
+        quantise_wa(2)
+        z_bf = sb.tile([P, U, PACK], BF16, name="z_bf", align_bytes=64)
 
-        g_rows = {t: sb.tile([P, H], F32, name="g%d" % t, tag="row%d" % t, align_bytes=64) for t in range(1, PACK)}
-        quantise_wa(0)
-        for n in range(PIECES):
-            if n + 1 < PIECES:
-                quantise_wa(n + 1)
-            tag = "piece%d" % (n + 1) if n + 1 < PIECES else "g0_last"
-            a, b = PIECE * n, PIECE * (n + 1)
-            g = sb.tile([P, PIECE], F32, name="g0", tag=tag, align_bytes=64)
-            project(0, a, b, n, g[:])
-            scatter(0, a, b, g)
-        for t in range(1, PACK):
-            project(t, 0, H, PIECES + t - 1, g_rows[t][:])
+        def weigh_on_scalar(t, a, b):
+            nc.scalar.activation(out=z_bf[:, a:b, t], in_=z32[t][:, a:b], func=COPY, scale=gt_sb[:, t : t + 1])
 
+        gs = [project(t, a, b, len(early) + n, tag) for n, (t, a, b, tag) in enumerate(late)]
+        for n, (t, a, b, tag) in enumerate(late):
+            scatter(t, a, b, gs[n])
+            if n == 0:
+                w1w = sb.tile([P, N], U32, name="w1w", tag="rounded2", align_bytes=64)
+                deal(nc.gpsimd, w1w[:], w1w_raw[:].bitcast(U32))
+                w1s = sb.tile([P, N], U8, name="w1s", tag="piece2", align_bytes=64)
+                deal(nc.gpsimd, w1s[:], w1s_raw[:])
+            if n == 1:
+                weigh_on_scalar(first, 0, U)
+            if n == 2:
+                nc.gpsimd.tensor_scalar(
+                    out=z_bf[:, :, second : second + 2],
+                    in0=z32[second][:].unsqueeze(2).to_broadcast([P, U, 2]),
+                    scalar1=gt_sb[:, second : second + 1],
+                    scalar2=0.0,
+                    op0=MULT,
+                    op1=ADD,
+                )
+            if n == 3:
+                weigh_on_scalar(third, 0, U // 2)
+                weigh_on_scalar(third, U // 2, U)
+        weigh_on_scalar(last, SCALAR_FROM, U)
 
         widths = [b - a for a, b in CHUNKS]
         cols = [slice(a, b) for a, b in CHUNKS]
         chunks = range(len(CHUNKS))
-        z_bf = sb.tile([P, U, PACK], BF16, name="z_bf", tag="xw_then_z", align_bytes=64)
-        last = PACK - 1
-
-        def weigh_on_scalar(dst, src, t):
-            nc.scalar.activation(out=dst, in_=src, func=COPY, scale=gt_sb[:, t : t + 1])
-
-        for t in range(PACK):
-            if t > 0:
-                scatter(t, 0, H, g_rows[t])
-            if t == 1:
-                w1w = sb.tile([P, N], U32, name="w1w", tag="row1", align_bytes=64)
-                deal_on_gpsimd(nc, w1w[:], w1w_raw[:].bitcast(U32))
-            if t == 2:
-                w1s = sb.tile([P, N], U8, name="w1s", tag="row2", align_bytes=64)
-                deal_on_gpsimd(nc, w1s[:], w1s_raw[:])
-            if t < last - 1:
-                weigh_on_scalar(z_bf[:, :, t], z32[t][:], t)
-            if t == last - 1:
-                for a, b in THIRD_ROW_SPANS:
-                    weigh_on_scalar(z_bf[:, a:b, t : t + 2], z32[t][:, a:b].unsqueeze(2).to_broadcast([P, b - a, 2]), t)
-
         z_w = [sb.tile([P, widths[c]], U32, name="z_w%d" % c, align_bytes=64) for c in chunks]
         z_s = [sb.tile([P, widths[c]], U8, name="z_s%d" % c, align_bytes=64) for c in chunks]
 
         def weigh_on_vector(c):
-            nc.vector.tensor_scalar(
-                out=z_bf[:, cols[c], last], in0=z32[last][:, cols[c]], scalar1=gt_sb[:, last : last + 1], scalar2=None, op0=MULT
-            )
+            a, b = CHUNKS[c][0], min(CHUNKS[c][1], SCALAR_FROM)
+            if a < b:
+                nc.vector.tensor_scalar(
+                    out=z_bf[:, a:b, last], in0=z32[last][:, a:b], scalar1=gt_sb[:, last : last + 1], scalar2=None, op0=MULT
+                )
 
         def quantise_z(c):
             nc.vector.quantize_mx(out=z_w[c][:].bitcast(FP8X4), scales=z_s[c][:], in_=z_bf[:, cols[c], :].rearrange("p c t -> p (c t)"))
@@ -190,7 +210,7 @@ def tile_picked_blkmix_gelu_po_kernel(
             here = slice(cols[c].start - spans[r].start, cols[c].stop - spans[r].start)
             per_bank = BANK // widths[c]
             for t0 in range(0, PACK, per_bank):
-                acc = ps.tile([P, per_bank, widths[c]], F32, name="acc", tag="bank%d" % (bank % 8))
+                acc = ps.tile([P, per_bank, widths[c]], F32, name="acc", tag="bank%d" % (bank % BANKS))
                 bank = bank + 1
                 for u in range(per_bank):
                     rows = slice(P * (t0 + u), P * (t0 + u + 1))
@@ -207,7 +227,7 @@ def tile_picked_blkmix_gelu_po_kernel(
                 nc.sync.dma_start(out=out_rows[:, t0 : t0 + per_bank, cols[c]], in_=o32[r][:, t0 : t0 + per_bank, here])
             return bank
 
-        bank = 7
+        bank = 0
         for r, (lo, hi) in enumerate(ROUNDS):
             for c in range(lo, hi):
                 bank = mix(r, c, bank)
@@ -219,8 +239,8 @@ def tile_picked_blkmix_gelu_po_kernel(
                     nc.vector.quantize_mx(
                         out=o_w[:, a:b].bitcast(FP8X4), scales=o_s[:, a:b], in_=o_bf[:, a:b, :].rearrange("p c t -> p (c t)")
                     )
-        for queue, a, b in ((nc.sync, 0, 640), (nc.sync, 640, 896), (nc.sync, 896, U)):
-            queue.dma_start(out=out_words[:, a:b], in_=o_w[:, a:b])
+        for a, b in WORD_STORES:
+            nc.sync.dma_start(out=out_words[:, a:b], in_=o_w[:, a:b])
         for q in range(QUADS):
             queue = nc.scalar if q % 2 else nc.sync
             queue.dma_start(out=out_2[0, 4 * q : 4 * q + 4, :].bitcast(I32), in_=o_s[32 * q : 32 * q + 4, :].bitcast(I32))

@@ -21,12 +21,9 @@ P = 128
 PACK = 4
 QUADS = 4
 BANK = 512
-BANKS = 8
 WA_PIECES = ((0, 128), (128, 256), (256, 512))
-CHUNKS = ((0, 128), (128, 384), (384, 640), (640, 896), (896, 1024))
-SCALAR_FROM = 768
-ROUNDS = ((0, 2), (2, 3), (3, 4), (4, 5))
-WORD_STORES = ((0, 640), (640, 896), (896, 1024))
+HALF = U // 2
+ON_VECTOR = ((0, 2),)
 
 
 def load_scale_rows(queue, plane, rows):
@@ -174,73 +171,79 @@ def tile_picked_blkmix_gelu_po_kernel(
             if n == 3:
                 weigh_on_scalar(third, 0, U // 2)
                 weigh_on_scalar(third, U // 2, U)
-        weigh_on_scalar(last, SCALAR_FROM, U)
 
-        widths = [b - a for a, b in CHUNKS]
-        cols = [slice(a, b) for a, b in CHUNKS]
-        chunks = range(len(CHUNKS))
-        z_w = [sb.tile([P, widths[c]], U32, name="z_w%d" % c, align_bytes=64) for c in chunks]
-        z_s = [sb.tile([P, widths[c]], U8, name="z_s%d" % c, align_bytes=64) for c in chunks]
+        z_w = [sb.tile([P, HALF], U32, name="z_w%d" % h, align_bytes=64) for h in range(2)]
+        z_s = [sb.tile([P, HALF], U8, name="z_s%d" % h, align_bytes=64) for h in range(2)]
 
-        def weigh_on_vector(c):
-            a, b = CHUNKS[c][0], min(CHUNKS[c][1], SCALAR_FROM)
-            if a < b:
-                nc.vector.tensor_scalar(
-                    out=z_bf[:, a:b, last], in0=z32[last][:, a:b], scalar1=gt_sb[:, last : last + 1], scalar2=None, op0=MULT
-                )
+        def weigh_on_vector(a, b):
+            nc.vector.tensor_scalar(
+                out=z_bf[:, a:b, last], in0=z32[last][:, a:b], scalar1=gt_sb[:, last : last + 1], scalar2=None, op0=MULT
+            )
 
-        def quantise_z(c):
-            nc.vector.quantize_mx(out=z_w[c][:].bitcast(FP8X4), scales=z_s[c][:], in_=z_bf[:, cols[c], :].rearrange("p c t -> p (c t)"))
+        def quantise_z(a, b):
+            h, lo, hi = a // HALF, a % HALF, (b - 1) % HALF + 1
+            nc.vector.quantize_mx(
+                out=z_w[h][:, lo:hi].bitcast(FP8X4), scales=z_s[h][:, lo:hi], in_=z_bf[:, a:b, :].rearrange("p c t -> p (c t)")
+            )
 
-        weigh_on_vector(0)
-        for c in chunks:
-            if c + 1 < len(CHUNKS):
-                weigh_on_vector(c + 1)
-            quantise_z(c)
+        weigh_on_scalar(last, 256, 512)
+        weigh_on_scalar(last, 768, 1024)
+        weigh_on_vector(0, 256)
+        weigh_on_vector(512, 640)
+        quantise_z(0, 256)
+        weigh_on_vector(640, 768)
+        quantise_z(256, 512)
+        quantise_z(512, 1024)
 
         out_rows = out_0.rearrange("(p t) n -> p t n", t=PACK)
         out_words = out_1[0].rearrange("p n t -> p (n t)").bitcast(I32)
         o_s = sb.tile([P, U], U8, name="o_s", align_bytes=64)
         o_w = sb.tile([P, U], I32, name="o_w", align_bytes=64)
         o_bf = sb.tile([P, U, PACK], BF16, name="o_bf", align_bytes=64)
-        spans = [slice(CHUNKS[lo][0], CHUNKS[hi - 1][1]) for lo, hi in ROUNDS]
-        o32 = [sb.tile([P, PACK, s.stop - s.start], F32, name="o32_%d" % s.start, align_bytes=64) for s in spans]
+        o32 = [sb.tile([P, PACK, HALF], F32, name="o32_%d" % h, align_bytes=64) for h in range(2)]
 
-        def mix(r, c, bank):
-            here = slice(cols[c].start - spans[r].start, cols[c].stop - spans[r].start)
-            per_bank = BANK // widths[c]
-            for t0 in range(0, PACK, per_bank):
-                acc = ps.tile([P, per_bank, widths[c]], F32, name="acc", tag="bank%d" % (bank % BANKS))
-                bank = bank + 1
-                for u in range(per_bank):
-                    rows = slice(P * (t0 + u), P * (t0 + u + 1))
-                    nc.tensor.matmul_mx(
-                        out=acc[:, u, :],
-                        lhsT=w1w[:, rows].bitcast(FP8X4),
-                        lhsT_scale=w1s[:, rows],
-                        rhs=z_w[c][:].bitcast(FP8X4),
-                        rhs_scale=z_s[c][:],
-                        start=True,
-                        stop=True,
-                    )
-                nc.scalar.copy(out=o32[r][:, t0 : t0 + per_bank, here], in_=acc[:])
-                nc.sync.dma_start(out=out_rows[:, t0 : t0 + per_bank, cols[c]], in_=o32[r][:, t0 : t0 + per_bank, here])
-            return bank
+        def mix(h, t):
+            acc = ps.tile([P, HALF], F32, name="acc", tag="bank%d" % (PACK * h + t))
+            rows = slice(P * t, P * (t + 1))
+            passes = ((0, 256), (256, 512)) if (h, t) == (0, 0) else ((0, HALF),)
+            for a, b in passes:
+                nc.tensor.matmul_mx(
+                    out=acc[:, a:b],
+                    lhsT=w1w[:, rows].bitcast(FP8X4),
+                    lhsT_scale=w1s[:, rows],
+                    rhs=z_w[h][:, a:b].bitcast(FP8X4),
+                    rhs_scale=z_s[h][:, a:b],
+                    start=True,
+                    stop=True,
+                )
+            if (h, t) in ON_VECTOR:
+                nc.vector.tensor_copy(out=o32[h][:, t, :], in_=acc[:])
+            else:
+                nc.scalar.copy(out=o32[h][:, t, :], in_=acc[:])
+            nc.sync.dma_start(out=out_rows[:, t, HALF * h : HALF * (h + 1)], in_=o32[h][:, t, :])
 
-        bank = 0
-        for r, (lo, hi) in enumerate(ROUNDS):
-            for c in range(lo, hi):
-                bank = mix(r, c, bank)
-        for r, span in enumerate(spans):
-            dst, src = interleave_views(o_bf[:, span, :], o32[r][:])
-            nc.vector.tensor_copy(out=dst, in_=src)
-            for a, b in CHUNKS:
-                if span.start <= a and b <= span.stop:
-                    nc.vector.quantize_mx(
-                        out=o_w[:, a:b].bitcast(FP8X4), scales=o_s[:, a:b], in_=o_bf[:, a:b, :].rearrange("p c t -> p (c t)")
-                    )
-        for a, b in WORD_STORES:
-            nc.sync.dma_start(out=out_words[:, a:b], in_=o_w[:, a:b])
+        def round_out(copy, a, b):
+            h, lo, hi = a // HALF, a % HALF, (b - 1) % HALF + 1
+            dst, src = interleave_views(o_bf[:, a:b, :], o32[h][:, :, lo:hi])
+            copy(out=dst, in_=src)
+
+        def quantise_out(a, b):
+            nc.vector.quantize_mx(out=o_w[:, a:b].bitcast(FP8X4), scales=o_s[:, a:b], in_=o_bf[:, a:b, :].rearrange("p c t -> p (c t)"))
+
+        for h in range(2):
+            for t in range(PACK):
+                mix(h, t)
+        round_out(nc.vector.tensor_copy, 0, 256)
+        round_out(nc.vector.tensor_copy, 256, 512)
+        quantise_out(0, 256)
+        quantise_out(256, 512)
+        nc.sync.dma_start(out=out_words[:, 0:512], in_=o_w[:, 0:512])
+        round_out(nc.scalar.copy, 896, 1024)
+        round_out(nc.vector.tensor_copy, 512, 768)
+        round_out(nc.vector.tensor_copy, 768, 896)
+        quantise_out(512, 768)
+        quantise_out(768, 1024)
+        nc.sync.dma_start(out=out_words[:, 512:1024], in_=o_w[:, 512:1024])
         for q in range(QUADS):
             queue = nc.scalar if q % 2 else nc.sync
             queue.dma_start(out=out_2[0, 4 * q : 4 * q + 4, :].bitcast(I32), in_=o_s[32 * q : 32 * q + 4, :].bitcast(I32))

@@ -23,7 +23,7 @@ QUADS = 4
 BANK = 512
 WA_PIECES = ((0, 128), (128, 256), (256, 512))
 HALF = U // 2
-ON_VECTOR = ((0, 2),)
+QUARTER = U // 4
 
 
 def load_scale_rows(queue, plane, rows):
@@ -155,8 +155,6 @@ def tile_picked_blkmix_gelu_po_kernel(
             if n == 0:
                 w1w = sb.tile([P, N], U32, name="w1w", tag="rounded2", align_bytes=64)
                 deal(nc.gpsimd, w1w[:], w1w_raw[:].bitcast(U32))
-                w1s = sb.tile([P, N], U8, name="w1s", tag="piece2", align_bytes=64)
-                deal(nc.gpsimd, w1s[:], w1s_raw[:])
             if n == 1:
                 weigh_on_scalar(first, 0, U)
             if n == 2:
@@ -168,6 +166,8 @@ def tile_picked_blkmix_gelu_po_kernel(
                     op0=MULT,
                     op1=ADD,
                 )
+                w1s = sb.tile([P, N], U8, name="w1s", tag="window_second", align_bytes=64)
+                deal(nc.gpsimd, w1s[:], w1s_raw[:])
             if n == 3:
                 weigh_on_scalar(third, 0, U // 2)
                 weigh_on_scalar(third, U // 2, U)
@@ -200,50 +200,74 @@ def tile_picked_blkmix_gelu_po_kernel(
         o_s = sb.tile([P, U], U8, name="o_s", align_bytes=64)
         o_w = sb.tile([P, U], I32, name="o_w", align_bytes=64)
         o_bf = sb.tile([P, U, PACK], BF16, name="o_bf", align_bytes=64)
-        o32 = [sb.tile([P, PACK, HALF], F32, name="o32_%d" % h, align_bytes=64) for h in range(2)]
+        o32 = sb.tile([P, PACK, U], F32, name="o32", align_bytes=64)
 
-        def mix(h, t):
-            acc = ps.tile([P, HALF], F32, name="acc", tag="bank%d" % (PACK * h + t))
-            rows = slice(P * t, P * (t + 1))
-            passes = ((0, 256), (256, 512)) if (h, t) == (0, 0) else ((0, HALF),)
-            for a, b in passes:
-                nc.tensor.matmul_mx(
-                    out=acc[:, a:b],
-                    lhsT=w1w[:, rows].bitcast(FP8X4),
-                    lhsT_scale=w1s[:, rows],
-                    rhs=z_w[h][:, a:b].bitcast(FP8X4),
-                    rhs_scale=z_s[h][:, a:b],
-                    start=True,
-                    stop=True,
-                )
-            if (h, t) in ON_VECTOR:
-                nc.vector.tensor_copy(out=o32[h][:, t, :], in_=acc[:])
-            else:
-                nc.scalar.copy(out=o32[h][:, t, :], in_=acc[:])
-            nc.sync.dma_start(out=out_rows[:, t, HALF * h : HALF * (h + 1)], in_=o32[h][:, t, :])
+        def warm_up(bank):
+            unread = ps.tile([P, BANK], F32, name="unread", tag="bank%d" % bank)
+            nc.tensor.matmul_mx(
+                out=unread[:],
+                lhsT=w1w[:, 0:P].bitcast(FP8X4),
+                lhsT_scale=w1s[:, 0:P],
+                rhs=wa_w[:].bitcast(FP8X4),
+                rhs_scale=wa_s[:],
+                start=True,
+                stop=True,
+            )
+
+        def mix(bank, copy, lanes, a, b):
+            h, lo, hi = a // HALF, a % HALF, (b - 1) % HALF + 1
+            acc = ps.tile([P, len(lanes), b - a], F32, name="acc", tag="bank%d" % bank)
+            step = QUARTER if h == 0 else HALF
+            for u, t in enumerate(lanes):
+                rows = slice(P * t, P * (t + 1))
+                for c in range(lo, hi, step):
+                    nc.tensor.matmul_mx(
+                        out=acc[:, u, c - lo : c - lo + step],
+                        lhsT=w1w[:, rows].bitcast(FP8X4),
+                        lhsT_scale=w1s[:, rows],
+                        rhs=z_w[h][:, c : c + step].bitcast(FP8X4),
+                        rhs_scale=z_s[h][:, c : c + step],
+                        start=True,
+                        stop=True,
+                    )
+            copy(out=o32[:, lanes[0] : lanes[-1] + 1, a:b], in_=acc[:])
+
+        def store(lanes, a, b):
+            nc.sync.dma_start(out=out_rows[:, lanes[0] : lanes[-1] + 1, a:b], in_=o32[:, lanes[0] : lanes[-1] + 1, a:b])
 
         def round_out(copy, a, b):
-            h, lo, hi = a // HALF, a % HALF, (b - 1) % HALF + 1
-            dst, src = interleave_views(o_bf[:, a:b, :], o32[h][:, :, lo:hi])
+            dst, src = interleave_views(o_bf[:, a:b, :], o32[:, :, a:b])
             copy(out=dst, in_=src)
 
         def quantise_out(a, b):
             nc.vector.quantize_mx(out=o_w[:, a:b].bitcast(FP8X4), scales=o_s[:, a:b], in_=o_bf[:, a:b, :].rearrange("p c t -> p (c t)"))
+            nc.sync.dma_start(out=out_words[:, a:b], in_=o_w[:, a:b])
 
-        for h in range(2):
-            for t in range(PACK):
-                mix(h, t)
-        round_out(nc.vector.tensor_copy, 0, 256)
-        round_out(nc.vector.tensor_copy, 256, 512)
-        quantise_out(0, 256)
-        quantise_out(256, 512)
-        nc.sync.dma_start(out=out_words[:, 0:512], in_=o_w[:, 0:512])
-        round_out(nc.scalar.copy, 896, 1024)
-        round_out(nc.vector.tensor_copy, 512, 768)
-        round_out(nc.vector.tensor_copy, 768, 896)
-        quantise_out(512, 768)
-        quantise_out(768, 1024)
-        nc.sync.dma_start(out=out_words[:, 512:1024], in_=o_w[:, 512:1024])
+        on_scalar, on_vector = nc.scalar.copy, nc.vector.tensor_copy
+        warm_up(6)
+        warm_up(7)
+        mix(0, on_scalar, (0,), 0, 256)
+        store((0,), 0, 256)
+        mix(1, on_scalar, (1,), 0, 256)
+        store((1,), 0, 256)
+        mix(2, on_scalar, (0, 1), 256, 512)
+        store((0, 1), 256, 512)
+        mix(3, on_vector, (2,), 0, 512)
+        mix(4, on_vector, (3,), 0, 512)
+        mix(5, on_scalar, (0,), 512, 1024)
+        store((0,), 512, 1024)
+        mix(6, on_vector, (2,), 512, 1024)
+        store((2,), 0, 1024)
+        mix(7, on_scalar, (1,), 512, 1024)
+        store((1,), 512, 1024)
+        mix(0, on_vector, (3,), 512, 1024)
+        store((3,), 0, 1024)
+        round_out(on_scalar, 0, 256)
+        round_out(on_scalar, 256, 512)
+        round_out(on_vector, 512, 768)
+        round_out(on_vector, 768, 1024)
+        quantise_out(512, 1024)
+        quantise_out(0, 512)
         for q in range(QUADS):
             queue = nc.scalar if q % 2 else nc.sync
             queue.dma_start(out=out_2[0, 4 * q : 4 * q + 4, :].bitcast(I32), in_=o_s[32 * q : 32 * q + 4, :].bitcast(I32))

@@ -24,6 +24,7 @@ BANK = 512
 WA_PIECES = ((0, 128), (128, 256), (256, 512))
 HALF = U // 2
 QUARTER = U // 4
+SCALAR_ROUNDS_FROM = 704
 
 
 def load_scale_rows(queue, plane, rows):
@@ -246,28 +247,24 @@ def tile_picked_blkmix_gelu_po_kernel(
         on_scalar, on_vector = nc.scalar.copy, nc.vector.tensor_copy
         warm_up(6)
         warm_up(7)
-        mix(0, on_scalar, (0,), 0, 256)
-        store((0,), 0, 256)
-        mix(1, on_scalar, (1,), 0, 256)
-        store((1,), 0, 256)
-        mix(2, on_scalar, (0, 1), 256, 512)
-        store((0, 1), 256, 512)
-        mix(3, on_vector, (2,), 0, 512)
-        mix(4, on_vector, (3,), 0, 512)
-        mix(5, on_scalar, (0,), 512, 1024)
+        for bank, (t, a, b) in enumerate(((0, 0, 256), (1, 0, 256), (0, 256, 512), (1, 256, 512))):
+            mix(bank, on_scalar, (t,), a, b)
+            store((t,), a, b)
+        mix(4, on_vector, (2,), 0, 512)
+        mix(5, on_vector, (3,), 0, 512)
+        mix(6, on_scalar, (0,), 512, 1024)
         store((0,), 512, 1024)
-        mix(6, on_vector, (2,), 512, 1024)
-        store((2,), 0, 1024)
         mix(7, on_scalar, (1,), 512, 1024)
         store((1,), 512, 1024)
+        on_vector(out=o_bf[:, 0:256, :], in_=o32[:, :, 0:256].rearrange("p t c -> p c t"))
         mix(0, on_vector, (3,), 512, 1024)
-        store((3,), 0, 1024)
-        round_out(on_scalar, 0, 256)
-        round_out(on_scalar, 256, 512)
-        round_out(on_vector, 512, 768)
-        round_out(on_vector, 768, 1024)
-        quantise_out(512, 1024)
+        mix(1, on_scalar, (2,), 512, 1024)
+        store((2, 3), 0, 1024)
+        round_out(on_scalar, SCALAR_ROUNDS_FROM, 1024)
+        round_out(on_vector, 256, 512)
+        round_out(on_vector, 512, SCALAR_ROUNDS_FROM)
         quantise_out(0, 512)
+        quantise_out(512, 1024)
         for q in range(QUADS):
             queue = nc.scalar if q % 2 else nc.sync
             queue.dma_start(out=out_2[0, 4 * q : 4 * q + 4, :].bitcast(I32), in_=o_s[32 * q : 32 * q + 4, :].bitcast(I32))

@@ -70,11 +70,15 @@ def tile_picked_blkmix_gelu_po_kernel(
             a, b = WA_PIECES[n]
             nc.sync.dma_start(out=wa_raw[n][:], in_=wa_rows[:, :, a:b])
 
+        def clear_window(engine, t, tag):
+            z32[t] = sb.tile([P, U], F32, name="z32_%d" % t, tag=tag, align_bytes=64)
+            engine.memset(z32[t][:], 0.0)
+
         nc.gpsimd.memset(xs_all[:].bitcast(I32), 0)
-        warm = sb.tile([P, 1], F32, name="warm")
-        nc.gpsimd.memset(warm[:], 0.0)
+        clear_window(nc.vector, first, "window_first")
         warmed = sb.tile([P, 1], F32, name="warmed")
-        nc.scalar.activation(out=warmed[:], in_=warm[:], func=GELU)
+        nc.scalar.activation(out=warmed[:], in_=z32[first][:, 0:1], func=GELU)
+        clear_window(nc.vector, second, "window_second")
         nc.sync.dma_start(offs_sb[:], offs)
         load_wa(0)
         load_scale_rows(nc.sync, xs_all, x_scales[0])
@@ -105,13 +109,6 @@ def tile_picked_blkmix_gelu_po_kernel(
         quantise_wa(0)
         nc.vector.tensor_copy(out=dealt_in_stream_order(xw[:]), in_=xw_all[:].bitcast(U32).indirect(offs_sb[:]))
         quantise_wa(1)
-
-        def clear_window(engine, t, tag):
-            z32[t] = sb.tile([P, U], F32, name="z32_%d" % t, tag=tag, align_bytes=64)
-            engine.memset(z32[t][:], 0.0)
-
-        clear_window(nc.vector, first, "window_first")
-        clear_window(nc.vector, second, "window_second")
         clear_window(nc.gpsimd, last, "rounded0")
         clear_window(nc.gpsimd, third, "rounded1")
 
@@ -147,8 +144,16 @@ def tile_picked_blkmix_gelu_po_kernel(
         quantise_wa(2)
         z_bf = sb.tile([P, U, PACK], BF16, name="z_bf", align_bytes=64)
 
+        w1s_lanes = w1s_raw[:].rearrange("p (m t) -> p t m", t=PACK)
+        factor = {t: gt_sb[:, t : t + 1] for t in (first, third)}
+
+        def set_factor_aside(t):
+            aside = sb.tile([P, 1], F32, name="gt_aside%d" % t, tag="gt_aside")
+            nc.gpsimd.tensor_copy(out=aside[:], in_=gt_sb[:, t : t + 1])
+            factor[t] = aside[:]
+
         def weigh_on_scalar(t, a, b):
-            nc.scalar.activation(out=z_bf[:, a:b, t], in_=z32[t][:, a:b], func=COPY, scale=gt_sb[:, t : t + 1])
+            nc.scalar.activation(out=z_bf[:, a:b, t], in_=z32[t][:, a:b], func=COPY, scale=factor[t])
 
         gs = [project(t, a, b, len(early) + n, tag) for n, (t, a, b, tag) in enumerate(late)]
         for n, (t, a, b, tag) in enumerate(late):
@@ -156,29 +161,29 @@ def tile_picked_blkmix_gelu_po_kernel(
             if n == 0:
                 w1w = sb.tile([P, N], U32, name="w1w", tag="rounded2", align_bytes=64)
                 deal(nc.gpsimd, w1w[:], w1w_raw[:].bitcast(U32))
+                w1s_early = sb.tile([P, 2, P], U8, name="w1s_early", tag="piece2", align_bytes=64)
+                nc.gpsimd.tensor_copy(out=w1s_early[:], in_=w1s_lanes[:, 0:2, :])
+                set_factor_aside(second)
             if n == 1:
                 weigh_on_scalar(first, 0, U)
             if n == 2:
                 nc.gpsimd.tensor_scalar(
-                    out=z_bf[:, :, second : second + 2],
-                    in0=z32[second][:].unsqueeze(2).to_broadcast([P, U, 2]),
-                    scalar1=gt_sb[:, second : second + 1],
-                    scalar2=0.0,
-                    op0=MULT,
-                    op1=ADD,
+                    out=z_bf[:, :, second], in0=z32[second][:], scalar1=factor[second], scalar2=0.0, op0=MULT, op1=ADD
                 )
-                w1s = sb.tile([P, N], U8, name="w1s", tag="window_second", align_bytes=64)
-                deal(nc.gpsimd, w1s[:], w1s_raw[:])
+                set_factor_aside(last)
+                w1s_late = sb.tile([P, 2, P], U8, name="w1s_late", tag="window_second", align_bytes=64)
+                nc.gpsimd.tensor_copy(out=w1s_late[:], in_=w1s_lanes[:, 2:PACK, :])
             if n == 3:
                 weigh_on_scalar(third, 0, U // 2)
                 weigh_on_scalar(third, U // 2, U)
 
+        w1s = [w1s_early[:, 0, :], w1s_early[:, 1, :], w1s_late[:, 0, :], w1s_late[:, 1, :]]
         z_w = [sb.tile([P, HALF], U32, name="z_w%d" % h, align_bytes=64) for h in range(2)]
         z_s = [sb.tile([P, HALF], U8, name="z_s%d" % h, align_bytes=64) for h in range(2)]
 
         def weigh_on_vector(a, b):
             nc.vector.tensor_scalar(
-                out=z_bf[:, a:b, last], in0=z32[last][:, a:b], scalar1=gt_sb[:, last : last + 1], scalar2=None, op0=MULT
+                out=z_bf[:, a:b, last], in0=z32[last][:, a:b], scalar1=factor[last], scalar2=None, op0=MULT
             )
 
         def quantise_z(a, b):
@@ -194,7 +199,8 @@ def tile_picked_blkmix_gelu_po_kernel(
         quantise_z(0, 256)
         weigh_on_vector(640, 768)
         quantise_z(256, 512)
-        quantise_z(512, 1024)
+        quantise_z(512, 768)
+        quantise_z(768, 1024)
 
         out_rows = out_0.rearrange("(p t) n -> p t n", t=PACK)
         out_words = out_1[0].rearrange("p n t -> p (n t)").bitcast(I32)
@@ -207,25 +213,24 @@ def tile_picked_blkmix_gelu_po_kernel(
             unread = ps.tile([P, BANK], F32, name="unread", tag="bank%d" % bank)
             nc.tensor.matmul_mx(
                 out=unread[:],
-                lhsT=w1w[:, 0:P].bitcast(FP8X4),
-                lhsT_scale=w1s[:, 0:P],
+                lhsT=w1w[:, P * last : P * (last + 1)].bitcast(FP8X4),
+                lhsT_scale=w1s[last],
                 rhs=wa_w[:].bitcast(FP8X4),
                 rhs_scale=wa_s[:],
                 start=True,
                 stop=True,
             )
 
-        def mix(bank, copy, lanes, a, b):
+        def mix(bank, copy, lanes, a, b, step):
             h, lo, hi = a // HALF, a % HALF, (b - 1) % HALF + 1
             acc = ps.tile([P, len(lanes), b - a], F32, name="acc", tag="bank%d" % bank)
-            step = QUARTER if h == 0 else HALF
             for u, t in enumerate(lanes):
                 rows = slice(P * t, P * (t + 1))
                 for c in range(lo, hi, step):
                     nc.tensor.matmul_mx(
                         out=acc[:, u, c - lo : c - lo + step],
                         lhsT=w1w[:, rows].bitcast(FP8X4),
-                        lhsT_scale=w1s[:, rows],
+                        lhsT_scale=w1s[t],
                         rhs=z_w[h][:, c : c + step].bitcast(FP8X4),
                         rhs_scale=z_s[h][:, c : c + step],
                         start=True,
@@ -248,17 +253,17 @@ def tile_picked_blkmix_gelu_po_kernel(
         warm_up(6)
         warm_up(7)
         for bank, (t, a, b) in enumerate(((0, 0, 256), (1, 0, 256), (0, 256, 512), (1, 256, 512))):
-            mix(bank, on_scalar, (t,), a, b)
+            mix(bank, on_scalar, (t,), a, b, QUARTER)
             store((t,), a, b)
-        mix(4, on_vector, (2,), 0, 512)
-        mix(5, on_vector, (3,), 0, 512)
-        mix(6, on_scalar, (0,), 512, 1024)
+        mix(4, on_vector, (2,), 0, 512, QUARTER)
+        mix(5, on_vector, (3,), 0, 512, HALF)
+        mix(6, on_scalar, (0,), 512, 1024, QUARTER)
         store((0,), 512, 1024)
-        mix(7, on_scalar, (1,), 512, 1024)
+        mix(7, on_scalar, (1,), 512, 1024, HALF)
         store((1,), 512, 1024)
         on_vector(out=o_bf[:, 0:256, :], in_=o32[:, :, 0:256].rearrange("p t c -> p c t"))
-        mix(0, on_vector, (3,), 512, 1024)
-        mix(1, on_scalar, (2,), 512, 1024)
+        mix(0, on_vector, (3,), 512, 1024, HALF)
+        mix(1, on_scalar, (2,), 512, 1024, HALF)
         store((2, 3), 0, 1024)
         round_out(on_scalar, SCALAR_ROUNDS_FROM, 1024)
         round_out(on_vector, 256, 512)

@@ -24,7 +24,7 @@ BANK = 512
 WA_PIECES = ((0, 128), (128, 256), (256, 512))
 HALF = U // 2
 QUARTER = U // 4
-SCALAR_ROUNDS_FROM = 704
+SCALAR_ROUNDS_FROM = 736
 
 
 def load_scale_rows(queue, plane, rows):
@@ -209,18 +209,6 @@ def tile_picked_blkmix_gelu_po_kernel(
         o_bf = sb.tile([P, U, PACK], BF16, name="o_bf", align_bytes=64)
         o32 = sb.tile([P, PACK, U], F32, name="o32", align_bytes=64)
 
-        def warm_up(bank):
-            unread = ps.tile([P, BANK], F32, name="unread", tag="bank%d" % bank)
-            nc.tensor.matmul_mx(
-                out=unread[:],
-                lhsT=w1w[:, P * last : P * (last + 1)].bitcast(FP8X4),
-                lhsT_scale=w1s[last],
-                rhs=wa_w[:].bitcast(FP8X4),
-                rhs_scale=wa_s[:],
-                start=True,
-                stop=True,
-            )
-
         def mix(bank, copy, lanes, a, b, step):
             h, lo, hi = a // HALF, a % HALF, (b - 1) % HALF + 1
             acc = ps.tile([P, len(lanes), b - a], F32, name="acc", tag="bank%d" % bank)
@@ -250,21 +238,22 @@ def tile_picked_blkmix_gelu_po_kernel(
             nc.sync.dma_start(out=out_words[:, a:b], in_=o_w[:, a:b])
 
         on_scalar, on_vector = nc.scalar.copy, nc.vector.tensor_copy
-        warm_up(6)
-        warm_up(7)
         for bank, (t, a, b) in enumerate(((0, 0, 256), (1, 0, 256), (0, 256, 512), (1, 256, 512))):
             mix(bank, on_scalar, (t,), a, b, QUARTER)
             store((t,), a, b)
-        mix(4, on_vector, (2,), 0, 512, QUARTER)
+        mix(4, on_scalar, (2,), 0, 512, QUARTER)
+        store((2,), 0, 512)
         mix(5, on_vector, (3,), 0, 512, HALF)
+        store((3,), 0, 512)
         mix(6, on_scalar, (0,), 512, 1024, QUARTER)
         store((0,), 512, 1024)
         mix(7, on_scalar, (1,), 512, 1024, HALF)
         store((1,), 512, 1024)
         on_vector(out=o_bf[:, 0:256, :], in_=o32[:, :, 0:256].rearrange("p t c -> p c t"))
         mix(0, on_vector, (3,), 512, 1024, HALF)
+        store((3,), 512, 1024)
         mix(1, on_scalar, (2,), 512, 1024, HALF)
-        store((2, 3), 0, 1024)
+        store((2,), 512, 1024)
         round_out(on_scalar, SCALAR_ROUNDS_FROM, 1024)
         round_out(on_vector, 256, 512)
         round_out(on_vector, 512, SCALAR_ROUNDS_FROM)

@@ -24,7 +24,7 @@ BANK = 512
 WA_PIECES = ((0, 128), (128, 256), (256, 512))
 HALF = U // 2
 QUARTER = U // 4
-SCALAR_ROUNDS_FROM = 736
+SCALAR_ROUNDS_FROM = 832
 
 
 def load_scale_rows(queue, plane, rows):
@@ -144,16 +144,18 @@ def tile_picked_blkmix_gelu_po_kernel(
         quantise_wa(2)
         z_bf = sb.tile([P, U, PACK], BF16, name="z_bf", align_bytes=64)
 
-        w1s_lanes = w1s_raw[:].rearrange("p (m t) -> p t m", t=PACK)
-        factor = {t: gt_sb[:, t : t + 1] for t in (first, third)}
+        factor = {t: gt_sb[:, t : t + 1] for t in range(PACK)}
 
-        def set_factor_aside(t):
-            aside = sb.tile([P, 1], F32, name="gt_aside%d" % t, tag="gt_aside")
+        def set_aside(t, tag):
+            aside = sb.tile([P, 1], F32, name="aside", tag=tag, align_bytes=64)
             nc.gpsimd.tensor_copy(out=aside[:], in_=gt_sb[:, t : t + 1])
-            factor[t] = aside[:]
+            return aside
 
-        def weigh_on_scalar(t, a, b):
-            nc.scalar.activation(out=z_bf[:, a:b, t], in_=z32[t][:, a:b], func=COPY, scale=factor[t])
+        def weigh_on_gpsimd(out, in0, scale):
+            nc.gpsimd.tensor_scalar(out=out, in0=in0, scalar1=scale, scalar2=0.0, op0=MULT, op1=ADD)
+
+        def weigh_on_scalar(t, a, b, scale):
+            nc.scalar.activation(out=z_bf[:, a:b, t], in_=z32[t][:, a:b], func=COPY, scale=scale)
 
         gs = [project(t, a, b, len(early) + n, tag) for n, (t, a, b, tag) in enumerate(late)]
         for n, (t, a, b, tag) in enumerate(late):
@@ -161,29 +163,31 @@ def tile_picked_blkmix_gelu_po_kernel(
             if n == 0:
                 w1w = sb.tile([P, N], U32, name="w1w", tag="rounded2", align_bytes=64)
                 deal(nc.gpsimd, w1w[:], w1w_raw[:].bitcast(U32))
-                w1s_early = sb.tile([P, 2, P], U8, name="w1s_early", tag="piece2", align_bytes=64)
-                nc.gpsimd.tensor_copy(out=w1s_early[:], in_=w1s_lanes[:, 0:2, :])
-                set_factor_aside(second)
+                w1s_dealt = sb.tile([P, N], U8, name="w1s_dealt", tag="piece2", align_bytes=64)
+                deal(nc.gpsimd, w1s_dealt[:], w1s_raw[:])
+                outer_factor = set_aside(second, "before_outer")
+                inner_factor = set_aside(second, "before_inner")
             if n == 1:
-                weigh_on_scalar(first, 0, U)
+                weigh_on_scalar(first, 0, U, factor[first])
             if n == 2:
-                nc.gpsimd.tensor_scalar(
-                    out=z_bf[:, :, second], in0=z32[second][:], scalar1=factor[second], scalar2=0.0, op0=MULT, op1=ADD
+                weigh_on_gpsimd(
+                    z_bf[:, :, second].rearrange("p (q c) -> p q c", q=4)[:, 0:4:3, :],
+                    z32[second][:].rearrange("p (q c) -> p q c", q=4)[:, 0:4:3, :],
+                    outer_factor[:],
                 )
-                set_factor_aside(last)
-                w1s_late = sb.tile([P, 2, P], U8, name="w1s_late", tag="window_second", align_bytes=64)
-                nc.gpsimd.tensor_copy(out=w1s_late[:], in_=w1s_lanes[:, 2:PACK, :])
+                early_factor = set_aside(last, "before_outer")
+                weigh_on_gpsimd(z_bf[:, 256:768, second], z32[second][:, 256:768], inner_factor[:])
+                late_factor = set_aside(last, "before_inner")
             if n == 3:
-                weigh_on_scalar(third, 0, U // 2)
-                weigh_on_scalar(third, U // 2, U)
+                weigh_on_scalar(third, 0, U // 2, factor[third])
+                weigh_on_scalar(third, U // 2, U, factor[third])
 
-        w1s = [w1s_early[:, 0, :], w1s_early[:, 1, :], w1s_late[:, 0, :], w1s_late[:, 1, :]]
         z_w = [sb.tile([P, HALF], U32, name="z_w%d" % h, align_bytes=64) for h in range(2)]
         z_s = [sb.tile([P, HALF], U8, name="z_s%d" % h, align_bytes=64) for h in range(2)]
 
-        def weigh_on_vector(a, b):
+        def weigh_on_vector(a, b, scale):
             nc.vector.tensor_scalar(
-                out=z_bf[:, a:b, last], in0=z32[last][:, a:b], scalar1=factor[last], scalar2=None, op0=MULT
+                out=z_bf[:, a:b, last], in0=z32[last][:, a:b], scalar1=scale, scalar2=None, op0=MULT
             )
 
         def quantise_z(a, b):
@@ -192,15 +196,15 @@ def tile_picked_blkmix_gelu_po_kernel(
                 out=z_w[h][:, lo:hi].bitcast(FP8X4), scales=z_s[h][:, lo:hi], in_=z_bf[:, a:b, :].rearrange("p c t -> p (c t)")
             )
 
-        weigh_on_scalar(last, 256, 512)
-        weigh_on_scalar(last, 768, 1024)
-        weigh_on_vector(0, 256)
-        weigh_on_vector(512, 640)
-        quantise_z(0, 256)
-        weigh_on_vector(640, 768)
+        weigh_on_scalar(last, 768, U, early_factor[:])
+        weigh_on_vector(0, 128, early_factor[:])
+        weigh_on_vector(128, 256, early_factor[:])
+        quantise_z(0, 128)
+        quantise_z(128, 256)
+        weigh_on_vector(256, 512, late_factor[:])
+        weigh_on_vector(512, 768, late_factor[:])
         quantise_z(256, 512)
-        quantise_z(512, 768)
-        quantise_z(768, 1024)
+        quantise_z(512, U)
 
         out_rows = out_0.rearrange("(p t) n -> p t n", t=PACK)
         out_words = out_1[0].rearrange("p n t -> p (n t)").bitcast(I32)
@@ -209,22 +213,24 @@ def tile_picked_blkmix_gelu_po_kernel(
         o_bf = sb.tile([P, U, PACK], BF16, name="o_bf", align_bytes=64)
         o32 = sb.tile([P, PACK, U], F32, name="o32", align_bytes=64)
 
-        def mix(bank, copy, lanes, a, b, step):
+        banks = {}
+
+        def multiply(bank, t, a, b, opens):
+            if a == opens:
+                banks[bank] = ps.tile([P, BANK], F32, name="acc", tag="bank%d" % bank)
             h, lo, hi = a // HALF, a % HALF, (b - 1) % HALF + 1
-            acc = ps.tile([P, len(lanes), b - a], F32, name="acc", tag="bank%d" % bank)
-            for u, t in enumerate(lanes):
-                rows = slice(P * t, P * (t + 1))
-                for c in range(lo, hi, step):
-                    nc.tensor.matmul_mx(
-                        out=acc[:, u, c - lo : c - lo + step],
-                        lhsT=w1w[:, rows].bitcast(FP8X4),
-                        lhsT_scale=w1s[t],
-                        rhs=z_w[h][:, c : c + step].bitcast(FP8X4),
-                        rhs_scale=z_s[h][:, c : c + step],
-                        start=True,
-                        stop=True,
-                    )
-            copy(out=o32[:, lanes[0] : lanes[-1] + 1, a:b], in_=acc[:])
+            nc.tensor.matmul_mx(
+                out=banks[bank][:, a - opens : b - opens],
+                lhsT=w1w[:, P * t : P * (t + 1)].bitcast(FP8X4),
+                lhsT_scale=w1s_dealt[:, P * t : P * (t + 1)],
+                rhs=z_w[h][:, lo:hi].bitcast(FP8X4),
+                rhs_scale=z_s[h][:, lo:hi],
+                start=True,
+                stop=True,
+            )
+
+        def empty(copy, bank, t, a, b):
+            copy(out=o32[:, t, a:b], in_=banks[bank][:, 0 : b - a])
 
         def store(lanes, a, b):
             nc.sync.dma_start(out=out_rows[:, lanes[0] : lanes[-1] + 1, a:b], in_=o32[:, lanes[0] : lanes[-1] + 1, a:b])
@@ -238,26 +244,36 @@ def tile_picked_blkmix_gelu_po_kernel(
             nc.sync.dma_start(out=out_words[:, a:b], in_=o_w[:, a:b])
 
         on_scalar, on_vector = nc.scalar.copy, nc.vector.tensor_copy
-        for bank, (t, a, b) in enumerate(((0, 0, 256), (1, 0, 256), (0, 256, 512), (1, 256, 512))):
-            mix(bank, on_scalar, (t,), a, b, QUARTER)
-            store((t,), a, b)
-        mix(4, on_scalar, (2,), 0, 512, QUARTER)
-        store((2,), 0, 512)
-        mix(5, on_vector, (3,), 0, 512, HALF)
-        store((3,), 0, 512)
-        mix(6, on_scalar, (0,), 512, 1024, QUARTER)
-        store((0,), 512, 1024)
-        mix(7, on_scalar, (1,), 512, 1024, HALF)
-        store((1,), 512, 1024)
+        for t in (0, 1):
+            multiply(t, t, 0, 128, 0)
+            empty(on_scalar, t, t, 0, 128)
+            store((t,), 0, 128)
+        for t in (2, 3):
+            multiply(t, t, 0, 128, 0)
+        for t in (0, 1):
+            multiply(4 + t, t, 128, 256, 128)
+            empty(on_scalar, 4 + t, t, 128, 256)
+            store((t,), 128, 256)
+        for t in (2, 3):
+            multiply(t, t, 128, 256, 0)
+            empty(on_scalar, t, t, 0, 256)
+            store((t,), 0, 256)
+        for t, bank, copy in ((0, 6, on_vector), (1, 7, on_scalar), (2, 0, on_vector), (3, 1, on_scalar)):
+            multiply(bank, t, 256, 512, 256)
+            empty(copy, bank, t, 256, 512)
+            if t % 2:
+                store((t - 1, t), 256, 512)
         on_vector(out=o_bf[:, 0:256, :], in_=o32[:, :, 0:256].rearrange("p t c -> p c t"))
-        mix(0, on_vector, (3,), 512, 1024, HALF)
-        store((3,), 512, 1024)
-        mix(1, on_scalar, (2,), 512, 1024, HALF)
-        store((2,), 512, 1024)
-        round_out(on_scalar, SCALAR_ROUNDS_FROM, 1024)
-        round_out(on_vector, 256, 512)
-        round_out(on_vector, 512, SCALAR_ROUNDS_FROM)
+        on_vector(out=o_bf[:, 256:512, :], in_=o32[:, :, 256:512].rearrange("p t c -> p c t"))
+        for t, bank, copy in ((0, 4, on_scalar), (1, 5, on_scalar), (3, 3, on_vector), (2, 2, on_scalar)):
+            multiply(bank, t, 512, 1024, 512)
+            empty(copy, bank, t, 512, 1024)
+            if t < 2:
+                store((t,), 512, 1024)
+        store((2, 3), 512, 1024)
         quantise_out(0, 512)
+        round_out(on_scalar, SCALAR_ROUNDS_FROM, 1024)
+        round_out(on_vector, 512, SCALAR_ROUNDS_FROM)
         quantise_out(512, 1024)
         for q in range(QUADS):
             queue = nc.scalar if q % 2 else nc.sync

@@ -19,7 +19,6 @@ ADD = mybir.AluOpType.add
 
 P = 128
 PACK = 4
-QUADS = 4
 BANK = 512
 WA_PIECES = ((0, 128), (128, 256), (256, 512))
 HALF = U // 2
@@ -28,8 +27,8 @@ SCALAR_ROUNDS_FROM = 832
 
 
 def load_scale_rows(queue, plane, rows):
-    for q in range(QUADS):
-        queue.dma_start(out=plane[32 * q : 32 * q + 4, :].bitcast(I32), in_=rows[4 * q : 4 * q + 4, :].bitcast(I32))
+    for r in range(4):
+        queue.dma_start(out=plane[r:P:32, :].bitcast(I32), in_=rows[r:16:4, :].bitcast(I32))
 
 
 def dealt_in_stream_order(dealt):
@@ -79,8 +78,8 @@ def tile_picked_blkmix_gelu_po_kernel(
         warmed = sb.tile([P, 1], F32, name="warmed")
         nc.scalar.activation(out=warmed[:], in_=z32[first][:, 0:1], func=GELU)
         clear_window(nc.vector, second, "window_second")
-        nc.sync.dma_start(offs_sb[:], offs)
         load_wa(0)
+        nc.sync.dma_start(offs_sb[:], offs)
         load_scale_rows(nc.sync, xs_all, x_scales[0])
         nc.sync.dma_start(out=xw_all[:], in_=x_words[0].rearrange("p n t -> p (n t)").bitcast(I32))
         load_wa(1)
@@ -91,7 +90,6 @@ def tile_picked_blkmix_gelu_po_kernel(
         nc.gpsimd.memset(w1s_raw[:].bitcast(I32), 0)
         load_scale_rows(nc.sync, w1s_raw, w1_scales[0])
 
-        xs_picked = sb.tile([P, S], U8, name="xs_picked", align_bytes=64)
         xs = sb.tile([P, S], U8, name="xs", align_bytes=64)
         xw = sb.tile([P, S], U32, name="xw", align_bytes=64)
         wa_w = sb.tile([P, H], U32, name="wa_w", align_bytes=64)
@@ -104,8 +102,7 @@ def tile_picked_blkmix_gelu_po_kernel(
             nc.scalar.copy(out=dst, in_=src)
             nc.vector.quantize_mx(out=wa_w[:, a:b].bitcast(FP8X4), scales=wa_s[:, a:b], in_=wa_bf[:].rearrange("p c t -> p (c t)"))
 
-        nc.vector.tensor_copy(out=xs_picked[:], in_=xs_all[:].indirect(offs_sb[:]))
-        deal(nc.vector, xs[:], xs_picked[:])
+        nc.vector.tensor_copy(out=dealt_in_stream_order(xs[:]), in_=xs_all[:].indirect(offs_sb[:]))
         quantise_wa(0)
         nc.vector.tensor_copy(out=dealt_in_stream_order(xw[:]), in_=xw_all[:].bitcast(U32).indirect(offs_sb[:]))
         quantise_wa(1)
@@ -275,6 +272,6 @@ def tile_picked_blkmix_gelu_po_kernel(
         round_out(on_scalar, SCALAR_ROUNDS_FROM, 1024)
         round_out(on_vector, 512, SCALAR_ROUNDS_FROM)
         quantise_out(512, 1024)
-        for q in range(QUADS):
-            queue = nc.scalar if q % 2 else nc.sync
-            queue.dma_start(out=out_2[0, 4 * q : 4 * q + 4, :].bitcast(I32), in_=o_s[32 * q : 32 * q + 4, :].bitcast(I32))
+        for r in range(4):
+            queue = nc.scalar if r % 2 else nc.sync
+            queue.dma_start(out=out_2[0, r:16:4, :].bitcast(I32), in_=o_s[r:P:32, :].bitcast(I32))

@@ -90,6 +90,7 @@ def tile_picked_blkmix_gelu_po_kernel(
         nc.gpsimd.memset(w1s_raw[:].bitcast(I32), 0)
         load_scale_rows(nc.sync, w1s_raw, w1_scales[0])
 
+        xs_picked = sb.tile([P, S], U8, name="xs_picked", align_bytes=64)
         xs = sb.tile([P, S], U8, name="xs", align_bytes=64)
         xw = sb.tile([P, S], U32, name="xw", align_bytes=64)
         wa_w = sb.tile([P, H], U32, name="wa_w", align_bytes=64)
@@ -102,7 +103,8 @@ def tile_picked_blkmix_gelu_po_kernel(
             nc.scalar.copy(out=dst, in_=src)
             nc.vector.quantize_mx(out=wa_w[:, a:b].bitcast(FP8X4), scales=wa_s[:, a:b], in_=wa_bf[:].rearrange("p c t -> p (c t)"))
 
-        nc.vector.tensor_copy(out=dealt_in_stream_order(xs[:]), in_=xs_all[:].indirect(offs_sb[:]))
+        nc.vector.tensor_copy(out=xs_picked[:], in_=xs_all[:].indirect(offs_sb[:]))
+        deal(nc.vector, xs[:], xs_picked[:])
         quantise_wa(0)
         nc.vector.tensor_copy(out=dealt_in_stream_order(xw[:]), in_=xw_all[:].bitcast(U32).indirect(offs_sb[:]))
         quantise_wa(1)

@@ -245,35 +245,29 @@ def tile_picked_blkmix_gelu_po_kernel(
         on_scalar, on_vector = nc.scalar.copy, nc.vector.tensor_copy
         for t in (0, 1):
             multiply(t, t, 0, 128, 0)
-            empty(on_scalar, t, t, 0, 128)
-            store((t,), 0, 128)
-        for t in (2, 3):
-            multiply(t, t, 0, 128, 0)
-        for t in (0, 1):
-            multiply(4 + t, t, 128, 256, 128)
-            empty(on_scalar, 4 + t, t, 128, 256)
-            store((t,), 128, 256)
-        for t in (2, 3):
-            multiply(t, t, 128, 256, 0)
+        for t in range(PACK):
+            multiply(t, t, 128 if t < 2 else 0, 256, 0)
             empty(on_scalar, t, t, 0, 256)
             store((t,), 0, 256)
-        for t, bank, copy in ((0, 6, on_vector), (1, 7, on_scalar), (2, 0, on_vector), (3, 1, on_scalar)):
-            multiply(bank, t, 256, 512, 256)
-            empty(copy, bank, t, 256, 512)
+        for t in range(PACK):
+            multiply(4 + t, t, 256, 512, 256)
+            empty(on_scalar if t % 2 else on_vector, 4 + t, t, 256, 512)
             if t % 2:
                 store((t - 1, t), 256, 512)
         on_vector(out=o_bf[:, 0:256, :], in_=o32[:, :, 0:256].rearrange("p t c -> p c t"))
         on_vector(out=o_bf[:, 256:512, :], in_=o32[:, :, 256:512].rearrange("p t c -> p c t"))
-        for t, bank, copy in ((0, 4, on_scalar), (1, 5, on_scalar), (3, 3, on_vector), (2, 2, on_scalar)):
-            multiply(bank, t, 512, 1024, 512)
-            empty(copy, bank, t, 512, 1024)
+        for t, copy in ((0, on_scalar), (1, on_scalar), (3, on_vector), (2, on_scalar)):
+            multiply(t, t, 512, 1024, 512)
+            empty(copy, t, t, 512, 1024)
             if t < 2:
                 store((t,), 512, 1024)
         store((2, 3), 512, 1024)
         quantise_out(0, 512)
         round_out(on_scalar, SCALAR_ROUNDS_FROM, 1024)
-        round_out(on_vector, 512, SCALAR_ROUNDS_FROM)
-        quantise_out(512, 1024)
+        round_out(on_vector, 512, 768)
+        round_out(on_vector, 768, SCALAR_ROUNDS_FROM)
+        quantise_out(512, 768)
+        quantise_out(768, 1024)
         for r in range(4):
             queue = nc.scalar if r % 2 else nc.sync
             queue.dma_start(out=out_2[0, r:16:4, :].bitcast(I32), in_=o_s[r:P:32, :].bitcast(I32))

@@ -21,6 +21,7 @@ P = 128
 PACK = 4
 BANK = 512
 WA_PIECES = ((0, 128), (128, 256), (256, 512))
+OUT_BLOCKS = ((0, 256), (256, 512), (512, 1024))
 HALF = U // 2
 QUARTER = U // 4
 SCALAR_ROUNDS_FROM = 832
@@ -210,7 +211,11 @@ def tile_picked_blkmix_gelu_po_kernel(
         o_s = sb.tile([P, U], U8, name="o_s", align_bytes=64)
         o_w = sb.tile([P, U], I32, name="o_w", align_bytes=64)
         o_bf = sb.tile([P, U, PACK], BF16, name="o_bf", align_bytes=64)
-        o32 = sb.tile([P, PACK, U], F32, name="o32", align_bytes=64)
+        o32 = {a: sb.tile([P, PACK, b - a], F32, name="o32_%d" % a, align_bytes=64) for a, b in OUT_BLOCKS}
+
+        def result(lo, hi, a, b):
+            start = max(s for s, e in OUT_BLOCKS if s <= a)
+            return o32[start][:, lo:hi, a - start : b - start]
 
         banks = {}
 
@@ -229,13 +234,13 @@ def tile_picked_blkmix_gelu_po_kernel(
             )
 
         def empty(copy, bank, t, a, b):
-            copy(out=o32[:, t, a:b], in_=banks[bank][:, 0 : b - a])
+            copy(out=result(t, t + 1, a, b), in_=banks[bank][:, 0 : b - a].unsqueeze(1))
 
         def store(lanes, a, b):
-            nc.sync.dma_start(out=out_rows[:, lanes[0] : lanes[-1] + 1, a:b], in_=o32[:, lanes[0] : lanes[-1] + 1, a:b])
+            nc.sync.dma_start(out=out_rows[:, lanes[0] : lanes[-1] + 1, a:b], in_=result(lanes[0], lanes[-1] + 1, a, b))
 
         def round_out(copy, a, b):
-            dst, src = interleave_views(o_bf[:, a:b, :], o32[:, :, a:b])
+            dst, src = interleave_views(o_bf[:, a:b, :], result(0, PACK, a, b))
             copy(out=dst, in_=src)
 
         def quantise_out(a, b):
@@ -254,8 +259,8 @@ def tile_picked_blkmix_gelu_po_kernel(
             empty(on_scalar if t % 2 else on_vector, 4 + t, t, 256, 512)
             if t % 2:
                 store((t - 1, t), 256, 512)
-        on_vector(out=o_bf[:, 0:256, :], in_=o32[:, :, 0:256].rearrange("p t c -> p c t"))
-        on_vector(out=o_bf[:, 256:512, :], in_=o32[:, :, 256:512].rearrange("p t c -> p c t"))
+        round_out(on_vector, 0, 256)
+        round_out(on_vector, 256, 512)
         for t, copy in ((0, on_scalar), (1, on_scalar), (3, on_vector), (2, on_scalar)):
             multiply(t, t, 512, 1024, 512)
             empty(copy, t, t, 512, 1024)

@@ -15,15 +15,14 @@ FP8X4 = mybir.dt.float8_e4m3fn_x4
 GELU = mybir.ActivationFunctionType.Gelu_apprx_tanh
 COPY = mybir.ActivationFunctionType.Copy
 MULT = mybir.AluOpType.mult
-ADD = mybir.AluOpType.add
 
 P = 128
-PACK = 4
+LANES = 4
 BANK = 512
 WA_PIECES = ((0, 128), (128, 256), (256, 512))
+DIRECT = 256
+DEAL_AFTER = 384
 OUT_BLOCKS = ((0, 256), (256, 512), (512, 1024))
-HALF = U // 2
-QUARTER = U // 4
 SCALAR_ROUNDS_FROM = 832
 
 
@@ -32,16 +31,12 @@ def load_scale_rows(queue, plane, rows):
         queue.dma_start(out=plane[r:P:32, :].bitcast(I32), in_=rows[r:16:4, :].bitcast(I32))
 
 
-def dealt_in_stream_order(dealt):
-    return dealt.rearrange("p (t m) -> p m t", t=PACK)
-
-
 def deal(engine, dealt, plain):
-    engine.tensor_copy(out=dealt.rearrange("p (t m) -> p t m", t=PACK), in_=plain.rearrange("p (m t) -> p t m", t=PACK))
+    engine.tensor_copy(out=dealt.rearrange("p (t m) -> p t m", t=LANES), in_=plain.rearrange("p (m t) -> p t m", t=LANES))
 
 
-def interleave_views(packed, rows):
-    return packed.rearrange("p (c i) t -> p c t i", i=4), rows.rearrange("p t (c i) -> p c t i", i=4)
+def interleave(copy, packed, rows):
+    copy(out=packed.rearrange("p (c i) t -> p c t i", i=4), in_=rows.rearrange("p t (c i) -> p c t i", i=4))
 
 
 def tile_picked_blkmix_gelu_po_kernel(
@@ -52,227 +47,207 @@ def tile_picked_blkmix_gelu_po_kernel(
         sb = ctx.enter_context(tc.tile_pool(name="sb", bufs=1))
         ps = ctx.enter_context(tc.psum_pool(name="ps", bufs=1))
 
-        offs_sb = sb.tile([P, S // 16], U16, name="offs_sb")
-        fl_sb = sb.tile([P, H // 16], U16, name="fl_sb")
-        xw_all = sb.tile([P, T], I32, name="xw_all", align_bytes=64)
-        xs_all = sb.tile([P, T], U8, name="xs_all", align_bytes=64)
-        w1w_raw = sb.tile([P, N], I32, name="w1w_raw", align_bytes=64)
-        w1s_raw = sb.tile([P, N], U8, name="w1s_raw", align_bytes=64)
-        gt_sb = sb.tile([P, PACK], F32, name="gt_sb")
-        wa_raw = [
-            sb.tile([P, PACK, b - a], F32, name="wa_raw%d" % n, tag="piece%d" % n, align_bytes=64) for n, (a, b) in enumerate(WA_PIECES)
-        ]
-        first, second, third, last = 0, 2, 1, 3
-        z32 = {}
-        wa_rows = wa.rearrange("(p j) c -> p j c", j=PACK)
+        def tile(shape, dtype, name, tag=None):
+            return sb.tile(shape, dtype, name=name, tag=tag or name, align_bytes=64)
+
+        def product(out, lhs_words, lhs_scales, rhs_words, rhs_scales):
+            nc.tensor.matmul_mx(
+                out=out,
+                lhsT=lhs_words.bitcast(FP8X4),
+                lhsT_scale=lhs_scales,
+                rhs=rhs_words.bitcast(FP8X4),
+                rhs_scale=rhs_scales,
+                start=True,
+                stop=True,
+            )
+
+        def quantise(words, scales, packed):
+            nc.vector.quantize_mx(out=words.bitcast(FP8X4), scales=scales, in_=packed.rearrange("p c t -> p (c t)"))
+
+        offs_sb = tile([P, S // 16], U16, "offs_sb")
+        fl_sb = tile([P, H // 16], U16, "fl_sb")
+        x_table = tile([P, T], I32, "x_table")
+        xs_table = tile([P, T], U8, "xs_table")
+        w1_raw = tile([P, N], I32, "w1_raw")
+        w1s_raw = tile([P, N], U8, "w1s_raw")
+        gt_sb = tile([P, LANES], F32, "gt_sb")
+        wa_raw = [tile([P, LANES, b - a], F32, "wa_raw%d" % n) for n, (a, b) in enumerate(WA_PIECES)]
+        wa_rows = wa.rearrange("(p j) c -> p j c", j=LANES)
+        window = {}
+
+        def clear_window(engine, t, tag):
+            window[t] = tile([P, U], F32, "window%d" % t, tag)
+            engine.memset(window[t][:], 0.0)
 
         def load_wa(n):
             a, b = WA_PIECES[n]
             nc.sync.dma_start(out=wa_raw[n][:], in_=wa_rows[:, :, a:b])
 
-        def clear_window(engine, t, tag):
-            z32[t] = sb.tile([P, U], F32, name="z32_%d" % t, tag=tag, align_bytes=64)
-            engine.memset(z32[t][:], 0.0)
-
-        nc.gpsimd.memset(xs_all[:].bitcast(I32), 0)
-        clear_window(nc.vector, first, "window_first")
-        warmed = sb.tile([P, 1], F32, name="warmed")
-        nc.scalar.activation(out=warmed[:], in_=z32[first][:, 0:1], func=GELU)
-        clear_window(nc.vector, second, "window_second")
+        nc.gpsimd.memset(xs_table[:].bitcast(I32), 0)
+        clear_window(nc.vector, 0, None)
+        warmed = tile([P, 1], F32, "warmed")
+        nc.scalar.activation(out=warmed[:], in_=window[0][:, 0:1], func=GELU)
+        clear_window(nc.vector, 1, None)
         load_wa(0)
         nc.sync.dma_start(offs_sb[:], offs)
-        load_scale_rows(nc.sync, xs_all, x_scales[0])
-        nc.sync.dma_start(out=xw_all[:], in_=x_words[0].rearrange("p n t -> p (n t)").bitcast(I32))
+        load_scale_rows(nc.sync, xs_table, x_scales[0])
+        nc.sync.dma_start(out=x_table[:], in_=x_words[0].rearrange("p n t -> p (n t)").bitcast(I32))
         load_wa(1)
         nc.sync.dma_start(fl_sb[:], fl)
         load_wa(2)
-        nc.sync.dma_start(out=w1w_raw[:], in_=w1_words[0].rearrange("p n t -> p (n t)").bitcast(I32))
-        nc.sync.dma_start(out=gt_sb[:], in_=gt.rearrange("(p t) o -> p (t o)", t=PACK))
+        nc.sync.dma_start(out=w1_raw[:], in_=w1_words[0].rearrange("p n t -> p (n t)").bitcast(I32))
+        nc.sync.dma_start(out=gt_sb[:], in_=gt.rearrange("(p t) o -> p (t o)", t=LANES))
         nc.gpsimd.memset(w1s_raw[:].bitcast(I32), 0)
         load_scale_rows(nc.sync, w1s_raw, w1_scales[0])
 
-        xs_picked = sb.tile([P, S], U8, name="xs_picked", align_bytes=64)
-        xs = sb.tile([P, S], U8, name="xs", align_bytes=64)
-        xw = sb.tile([P, S], U32, name="xw", align_bytes=64)
-        wa_w = sb.tile([P, H], U32, name="wa_w", align_bytes=64)
-        wa_s = sb.tile([P, H], U8, name="wa_s", align_bytes=64)
+        xs_picked = tile([P, S], U8, "xs_picked")
+        xs = tile([P, S], U8, "xs")
+        xw = tile([P, S], U32, "xw")
+        wa_w = tile([P, H], U32, "wa_w")
+        wa_s = tile([P, H], U8, "wa_s")
 
         def quantise_wa(n):
             a, b = WA_PIECES[n]
-            wa_bf = sb.tile([P, b - a, PACK], BF16, name="wa_bf%d" % n, tag="rounded%d" % n, align_bytes=64)
-            dst, src = interleave_views(wa_bf[:], wa_raw[n][:])
-            nc.scalar.copy(out=dst, in_=src)
-            nc.vector.quantize_mx(out=wa_w[:, a:b].bitcast(FP8X4), scales=wa_s[:, a:b], in_=wa_bf[:].rearrange("p c t -> p (c t)"))
+            rounded = tile([P, b - a, LANES], BF16, "wa_bf%d" % n)
+            interleave(nc.scalar.copy, rounded[:], wa_raw[n][:])
+            quantise(wa_w[:, a:b], wa_s[:, a:b], rounded[:])
 
-        nc.vector.tensor_copy(out=xs_picked[:], in_=xs_all[:].indirect(offs_sb[:]))
+        nc.vector.tensor_copy(out=xs_picked[:], in_=xs_table[:].indirect(offs_sb[:]))
         deal(nc.vector, xs[:], xs_picked[:])
         quantise_wa(0)
-        nc.vector.tensor_copy(out=dealt_in_stream_order(xw[:]), in_=xw_all[:].bitcast(U32).indirect(offs_sb[:]))
+        nc.vector.tensor_copy(out=xw[:].rearrange("p (t m) -> p m t", t=LANES), in_=x_table[:].bitcast(U32).indirect(offs_sb[:]))
         quantise_wa(1)
-        clear_window(nc.gpsimd, last, "rounded0")
-        clear_window(nc.gpsimd, third, "rounded1")
+        clear_window(nc.gpsimd, 3, "wa_bf0")
+        clear_window(nc.gpsimd, 2, "wa_bf1")
 
-        def project(t, a, b, bank, tag):
-            y = ps.tile([P, BANK], F32, name="y", tag="bank%d" % bank)
-            tok = slice(P * t, P * (t + 1))
-            nc.tensor.matmul_mx(
-                out=y[:, 0 : b - a],
-                lhsT=xw[:, tok].bitcast(FP8X4),
-                lhsT_scale=xs[:, tok],
-                rhs=wa_w[:, a:b].bitcast(FP8X4),
-                rhs_scale=wa_s[:, a:b],
-                start=True,
-                stop=True,
-            )
-            g = sb.tile([P, b - a], F32, name="g", tag=tag, align_bytes=64)
-            nc.scalar.activation(out=g[:], in_=y[:, 0 : b - a], func=GELU)
+        def project(n, t, a, b, tag):
+            y = ps.tile([P, b - a], F32, name="y", tag="bank%d" % n)
+            tokens = slice(P * t, P * (t + 1))
+            product(y[:], xw[:, tokens], xs[:, tokens], wa_w[:, a:b], wa_s[:, a:b])
+            g = tile([P, b - a], F32, "g%d" % n, tag)
+            nc.scalar.activation(out=g[:], in_=y[:], func=GELU)
             return g
 
         def scatter(t, a, b, g):
-            nc.vector.tensor_copy(out=z32[t][:].indirect(fl_sb[:, a // 16 : b // 16]), in_=g[:])
+            nc.vector.tensor_copy(out=window[t][:].indirect(fl_sb[:, a // 16 : b // 16]), in_=g[:])
 
-        early = ((first, 0, 128, "piece1"), (second, 0, 256, "g1"), (first, 128, 256, "g2"))
-        late = (
-            (third, 0, 256, "piece2"),
-            (first, 256, 512, "g4"),
-            (second, 256, 512, "g5"),
-            (third, 256, 512, "g6"),
-            (last, 0, 512, "g7"),
-        )
+        z_bf = tile([P, U, LANES], BF16, "z_bf")
+        pairs = tile([P, 2, U - DIRECT, 2], BF16, "pairs")
+
+        def weigh_direct(t, weight):
+            nc.scalar.activation(out=z_bf[:, 0:DIRECT, t], in_=window[t][:, 0:DIRECT], func=COPY, scale=weight)
+
+        def weigh_paired(t, a, b, weight):
+            nc.scalar.activation(out=pairs[:, t // 2, a - DIRECT : b - DIRECT, t % 2], in_=window[t][:, a:b], func=COPY, scale=weight)
+
+        def weight_copy(t, tag):
+            weight = tile([P, 1], F32, tag + "%d" % t, tag)
+            nc.gpsimd.tensor_copy(out=weight[:], in_=gt_sb[:, t : t + 1])
+            return weight[:]
+
+        early = ((0, 0, 128, "wa_raw1"), (1, 0, 256, None), (0, 128, 256, None))
+        late = ((2, 0, 256, "wa_raw2"), (0, 256, H, None), (1, 256, H, None), (2, 256, H, None), (3, 0, H, None))
         for n, (t, a, b, tag) in enumerate(early):
-            scatter(t, a, b, project(t, a, b, n, tag))
+            scatter(t, a, b, project(n, t, a, b, tag))
         quantise_wa(2)
-        z_bf = sb.tile([P, U, PACK], BF16, name="z_bf", align_bytes=64)
+        activated = [project(len(early) + n, t, a, b, tag) for n, (t, a, b, tag) in enumerate(late)]
+        for (t, a, b, tag), g in zip(late, activated):
+            scatter(t, a, b, g)
+            if b == H and t < LANES - 1:
+                weight = gt_sb[:, t : t + 1]
+                weigh_direct(t, weight_copy(t, "direct") if t == 2 else weight)
+                weigh_paired(t, DIRECT, DEAL_AFTER, weight_copy(t, "paired") if t == 2 else weight)
+                weigh_paired(t, DEAL_AFTER, U, weight)
+        w1s = tile([P, N], U8, "w1s", "wa_raw2")
+        deal(nc.gpsimd, w1s[:], w1s_raw[:])
 
-        factor = {t: gt_sb[:, t : t + 1] for t in range(PACK)}
+        z_w = tile([P, U], U32, "z_w")
+        z_s = tile([P, U], U8, "z_s")
+        last_weight = weight_copy(LANES - 1, "direct")
+        w1w = tile([P, N], U32, "w1w", "paired")
+        deal(nc.gpsimd, w1w[:], w1_raw[:].bitcast(U32))
 
-        def set_aside(t, tag):
-            aside = sb.tile([P, 1], F32, name="aside", tag=tag, align_bytes=64)
-            nc.gpsimd.tensor_copy(out=aside[:], in_=gt_sb[:, t : t + 1])
-            return aside
-
-        def weigh_on_gpsimd(out, in0, scale):
-            nc.gpsimd.tensor_scalar(out=out, in0=in0, scalar1=scale, scalar2=0.0, op0=MULT, op1=ADD)
-
-        def weigh_on_scalar(t, a, b, scale):
-            nc.scalar.activation(out=z_bf[:, a:b, t], in_=z32[t][:, a:b], func=COPY, scale=scale)
-
-        gs = [project(t, a, b, len(early) + n, tag) for n, (t, a, b, tag) in enumerate(late)]
-        for n, (t, a, b, tag) in enumerate(late):
-            scatter(t, a, b, gs[n])
-            if n == 0:
-                w1w = sb.tile([P, N], U32, name="w1w", tag="rounded2", align_bytes=64)
-                deal(nc.gpsimd, w1w[:], w1w_raw[:].bitcast(U32))
-                w1s_dealt = sb.tile([P, N], U8, name="w1s_dealt", tag="piece2", align_bytes=64)
-                deal(nc.gpsimd, w1s_dealt[:], w1s_raw[:])
-                outer_factor = set_aside(second, "before_outer")
-                inner_factor = set_aside(second, "before_inner")
-            if n == 1:
-                weigh_on_scalar(first, 0, U, factor[first])
-            if n == 2:
-                weigh_on_gpsimd(
-                    z_bf[:, :, second].rearrange("p (q c) -> p q c", q=4)[:, 0:4:3, :],
-                    z32[second][:].rearrange("p (q c) -> p q c", q=4)[:, 0:4:3, :],
-                    outer_factor[:],
-                )
-                early_factor = set_aside(last, "before_outer")
-                weigh_on_gpsimd(z_bf[:, 256:768, second], z32[second][:, 256:768], inner_factor[:])
-                late_factor = set_aside(last, "before_inner")
-            if n == 3:
-                weigh_on_scalar(third, 0, U // 2, factor[third])
-                weigh_on_scalar(third, U // 2, U, factor[third])
-
-        z_w = [sb.tile([P, HALF], U32, name="z_w%d" % h, align_bytes=64) for h in range(2)]
-        z_s = [sb.tile([P, HALF], U8, name="z_s%d" % h, align_bytes=64) for h in range(2)]
-
-        def weigh_on_vector(a, b, scale):
-            nc.vector.tensor_scalar(
-                out=z_bf[:, a:b, last], in0=z32[last][:, a:b], scalar1=scale, scalar2=None, op0=MULT
+        def weave(a, b):
+            nc.vector.tensor_copy(
+                out=z_bf[:, a:b, :].rearrange("p c (h e) -> p c h e", h=2),
+                in_=pairs[:, :, a - DIRECT : b - DIRECT, :].rearrange("p h c e -> p c h e"),
             )
 
         def quantise_z(a, b):
-            h, lo, hi = a // HALF, a % HALF, (b - 1) % HALF + 1
-            nc.vector.quantize_mx(
-                out=z_w[h][:, lo:hi].bitcast(FP8X4), scales=z_s[h][:, lo:hi], in_=z_bf[:, a:b, :].rearrange("p c t -> p (c t)")
-            )
+            quantise(z_w[:, a:b], z_s[:, a:b], z_bf[:, a:b, :])
 
-        weigh_on_scalar(last, 768, U, early_factor[:])
-        weigh_on_vector(0, 128, early_factor[:])
-        weigh_on_vector(128, 256, early_factor[:])
+        for a in range(DIRECT, U, 256):
+            weigh_paired(LANES - 1, a, a + 256, gt_sb[:, LANES - 1 : LANES])
+        for a in (0, 128):
+            nc.vector.tensor_scalar(
+                out=z_bf[:, a : a + 128, LANES - 1],
+                in0=window[LANES - 1][:, a : a + 128],
+                scalar1=last_weight,
+                scalar2=None,
+                op0=MULT,
+            )
         quantise_z(0, 128)
         quantise_z(128, 256)
-        weigh_on_vector(256, 512, late_factor[:])
-        weigh_on_vector(512, 768, late_factor[:])
+        weave(256, 512)
+        weave(512, 768)
         quantise_z(256, 512)
-        quantise_z(512, U)
+        weave(768, U)
+        quantise_z(512, 768)
+        quantise_z(768, U)
 
-        out_rows = out_0.rearrange("(p t) n -> p t n", t=PACK)
+        out_rows = out_0.rearrange("(p t) n -> p t n", t=LANES)
         out_words = out_1[0].rearrange("p n t -> p (n t)").bitcast(I32)
-        o_s = sb.tile([P, U], U8, name="o_s", align_bytes=64)
-        o_w = sb.tile([P, U], I32, name="o_w", align_bytes=64)
-        o_bf = sb.tile([P, U, PACK], BF16, name="o_bf", align_bytes=64)
-        o32 = {a: sb.tile([P, PACK, b - a], F32, name="o32_%d" % a, align_bytes=64) for a, b in OUT_BLOCKS}
+        result = {a: tile([P, LANES, b - a], F32, "result%d" % a) for a, b in OUT_BLOCKS}
+        o_bf = tile([P, U, LANES], BF16, "o_bf")
+        o_w = tile([P, U], I32, "o_w")
+        o_s = tile([P, U], U8, "o_s")
+        acc = {}
 
-        def result(lo, hi, a, b):
-            start = max(s for s, e in OUT_BLOCKS if s <= a)
-            return o32[start][:, lo:hi, a - start : b - start]
-
-        banks = {}
-
-        def multiply(bank, t, a, b, opens):
-            if a == opens:
-                banks[bank] = ps.tile([P, BANK], F32, name="acc", tag="bank%d" % bank)
-            h, lo, hi = a // HALF, a % HALF, (b - 1) % HALF + 1
-            nc.tensor.matmul_mx(
-                out=banks[bank][:, a - opens : b - opens],
-                lhsT=w1w[:, P * t : P * (t + 1)].bitcast(FP8X4),
-                lhsT_scale=w1s_dealt[:, P * t : P * (t + 1)],
-                rhs=z_w[h][:, lo:hi].bitcast(FP8X4),
-                rhs_scale=z_s[h][:, lo:hi],
-                start=True,
-                stop=True,
-            )
+        def mix(bank, t, a, b, start):
+            if a == start:
+                acc[bank] = ps.tile([P, BANK], F32, name="acc", tag="bank%d" % bank)
+            rows = slice(P * t, P * (t + 1))
+            product(acc[bank][:, a - start : b - start], w1w[:, rows], w1s[:, rows], z_w[:, a:b], z_s[:, a:b])
 
         def empty(copy, bank, t, a, b):
-            copy(out=result(t, t + 1, a, b), in_=banks[bank][:, 0 : b - a].unsqueeze(1))
+            copy(out=result[a][:, t, :], in_=acc[bank][:, 0 : b - a])
 
-        def store(lanes, a, b):
-            nc.sync.dma_start(out=out_rows[:, lanes[0] : lanes[-1] + 1, a:b], in_=result(lanes[0], lanes[-1] + 1, a, b))
+        def store(lo, hi, a, b):
+            nc.sync.dma_start(out=out_rows[:, lo:hi, a:b], in_=result[a][:, lo:hi, :])
 
-        def round_out(copy, a, b):
-            dst, src = interleave_views(o_bf[:, a:b, :], result(0, PACK, a, b))
-            copy(out=dst, in_=src)
+        def round_on_vector(start, a, b):
+            nc.vector.tensor_copy(out=o_bf[:, a:b, :], in_=result[start][:, :, a - start : b - start].rearrange("p t c -> p c t"))
 
         def quantise_out(a, b):
-            nc.vector.quantize_mx(out=o_w[:, a:b].bitcast(FP8X4), scales=o_s[:, a:b], in_=o_bf[:, a:b, :].rearrange("p c t -> p (c t)"))
+            quantise(o_w[:, a:b], o_s[:, a:b], o_bf[:, a:b, :])
             nc.sync.dma_start(out=out_words[:, a:b], in_=o_w[:, a:b])
 
         on_scalar, on_vector = nc.scalar.copy, nc.vector.tensor_copy
         for t in (0, 1):
-            multiply(t, t, 0, 128, 0)
-        for t in range(PACK):
-            multiply(t, t, 128 if t < 2 else 0, 256, 0)
+            mix(t, t, 0, 128, 0)
+        for t in range(LANES):
+            mix(t, t, 128 if t < 2 else 0, 256, 0)
             empty(on_scalar, t, t, 0, 256)
-            store((t,), 0, 256)
-        for t in range(PACK):
-            multiply(4 + t, t, 256, 512, 256)
+            store(t, t + 1, 0, 256)
+        for t in range(LANES):
+            mix(4 + t, t, 256, 512, 256)
             empty(on_scalar if t % 2 else on_vector, 4 + t, t, 256, 512)
             if t % 2:
-                store((t - 1, t), 256, 512)
-        round_out(on_vector, 0, 256)
-        round_out(on_vector, 256, 512)
+                store(t - 1, t + 1, 256, 512)
+        round_on_vector(0, 0, 256)
+        round_on_vector(256, 256, 512)
         for t, copy in ((0, on_scalar), (1, on_scalar), (3, on_vector), (2, on_scalar)):
-            multiply(t, t, 512, 1024, 512)
-            empty(copy, t, t, 512, 1024)
+            mix(t, t, 512, U, 512)
+            empty(copy, t, t, 512, U)
             if t < 2:
-                store((t,), 512, 1024)
-        store((2, 3), 512, 1024)
+                store(t, t + 1, 512, U)
+        store(2, LANES, 512, U)
         quantise_out(0, 512)
-        round_out(on_scalar, SCALAR_ROUNDS_FROM, 1024)
-        round_out(on_vector, 512, 768)
-        round_out(on_vector, 768, SCALAR_ROUNDS_FROM)
+        interleave(on_scalar, o_bf[:, SCALAR_ROUNDS_FROM:U, :], result[512][:, :, SCALAR_ROUNDS_FROM - 512 :])
+        round_on_vector(512, 512, 768)
+        round_on_vector(512, 768, SCALAR_ROUNDS_FROM)
         quantise_out(512, 768)
-        quantise_out(768, 1024)
+        quantise_out(768, U)
         for r in range(4):
             queue = nc.scalar if r % 2 else nc.sync
             queue.dma_start(out=out_2[0, r:16:4, :].bitcast(I32), in_=o_s[r:P:32, :].bitcast(I32))

@@ -223,6 +223,8 @@ def tile_picked_blkmix_gelu_po_kernel(
             nc.sync.dma_start(out=out_words[:, a:b], in_=o_w[:, a:b])
 
         on_scalar, on_vector = nc.scalar.copy, nc.vector.tensor_copy
+        unread = ps.tile([P, BANK], F32, name="unread", tag="bank7")
+        product(unread[:], w1w[:, 0:P], w1s[:, 0:P], wa_w[:], wa_s[:])
         for t in (0, 1):
             mix(t, t, 0, 128, 0)
         for t in range(LANES):

@@ -22,7 +22,6 @@ BANK = 512
 WA_PIECES = ((0, 128), (128, 256), (256, 512))
 DIRECT = 256
 DEAL_AFTER = 384
-OUT_BLOCKS = ((0, 256), (256, 512), (512, 1024))
 SCALAR_ROUNDS_FROM = 832
 
 
@@ -197,7 +196,7 @@ def tile_picked_blkmix_gelu_po_kernel(
 
         out_rows = out_0.rearrange("(p t) n -> p t n", t=LANES)
         out_words = out_1[0].rearrange("p n t -> p (n t)").bitcast(I32)
-        result = {a: tile([P, LANES, b - a], F32, "result%d" % a) for a, b in OUT_BLOCKS}
+        result = tile([P, LANES, U], F32, "result")
         o_bf = tile([P, U, LANES], BF16, "o_bf")
         o_w = tile([P, U], I32, "o_w")
         o_s = tile([P, U], U8, "o_s")
@@ -210,13 +209,16 @@ def tile_picked_blkmix_gelu_po_kernel(
             product(acc[bank][:, a - start : b - start], w1w[:, rows], w1s[:, rows], z_w[:, a:b], z_s[:, a:b])
 
         def empty(copy, bank, t, a, b):
-            copy(out=result[a][:, t, :], in_=acc[bank][:, 0 : b - a])
+            copy(out=result[:, t, a:b], in_=acc[bank][:, 0 : b - a])
 
         def store(lo, hi, a, b):
-            nc.sync.dma_start(out=out_rows[:, lo:hi, a:b], in_=result[a][:, lo:hi, :])
+            nc.sync.dma_start(out=out_rows[:, lo:hi, a:b], in_=result[:, lo:hi, a:b])
 
-        def round_on_vector(start, a, b):
-            nc.vector.tensor_copy(out=o_bf[:, a:b, :], in_=result[start][:, :, a - start : b - start].rearrange("p t c -> p c t"))
+        def round_early(a, b):
+            nc.vector.tensor_copy(out=o_bf[:, a:b, :], in_=result[:, :, a:b].rearrange("p t c -> p c t"))
+
+        def round_late(copy, a, b):
+            interleave(copy, o_bf[:, a:b, :], result[:, :, a:b])
 
         def quantise_out(a, b):
             quantise(o_w[:, a:b], o_s[:, a:b], o_bf[:, a:b, :])
@@ -236,8 +238,8 @@ def tile_picked_blkmix_gelu_po_kernel(
             empty(on_scalar if t % 2 else on_vector, 4 + t, t, 256, 512)
             if t % 2:
                 store(t - 1, t + 1, 256, 512)
-        round_on_vector(0, 0, 256)
-        round_on_vector(256, 256, 512)
+        round_early(0, 256)
+        round_early(256, 512)
         for t, copy in ((0, on_scalar), (1, on_scalar), (3, on_vector), (2, on_scalar)):
             mix(t, t, 512, U, 512)
             empty(copy, t, t, 512, U)
@@ -245,9 +247,9 @@ def tile_picked_blkmix_gelu_po_kernel(
                 store(t, t + 1, 512, U)
         store(2, LANES, 512, U)
         quantise_out(0, 512)
-        interleave(on_scalar, o_bf[:, SCALAR_ROUNDS_FROM:U, :], result[512][:, :, SCALAR_ROUNDS_FROM - 512 :])
-        round_on_vector(512, 512, 768)
-        round_on_vector(512, 768, SCALAR_ROUNDS_FROM)
+        round_late(on_scalar, SCALAR_ROUNDS_FROM, U)
+        round_late(on_vector, 512, 768)
+        round_late(on_vector, 768, SCALAR_ROUNDS_FROM)
         quantise_out(512, 768)
         quantise_out(768, U)
         for r in range(4):

@@ -15,12 +15,14 @@ FP8X4 = mybir.dt.float8_e4m3fn_x4
 GELU = mybir.ActivationFunctionType.Gelu_apprx_tanh
 COPY = mybir.ActivationFunctionType.Copy
 MULT = mybir.AluOpType.mult
+ADD = mybir.AluOpType.add
 
 P = 128
 LANES = 4
 BANK = 512
 WA_PIECES = ((0, 128), (128, 256), (256, 512))
 DIRECT = 256
+PAIRED_END = 768
 DEAL_AFTER = 384
 SCALAR_ROUNDS_FROM = 832
 
@@ -131,10 +133,10 @@ def tile_picked_blkmix_gelu_po_kernel(
             nc.vector.tensor_copy(out=window[t][:].indirect(fl_sb[:, a // 16 : b // 16]), in_=g[:])
 
         z_bf = tile([P, U, LANES], BF16, "z_bf")
-        pairs = tile([P, 2, U - DIRECT, 2], BF16, "pairs")
+        pairs = tile([P, 2, PAIRED_END - DIRECT, 2], BF16, "pairs")
 
-        def weigh_direct(t, weight):
-            nc.scalar.activation(out=z_bf[:, 0:DIRECT, t], in_=window[t][:, 0:DIRECT], func=COPY, scale=weight)
+        def weigh_direct(t, a, b, weight):
+            nc.scalar.activation(out=z_bf[:, a:b, t], in_=window[t][:, a:b], func=COPY, scale=weight)
 
         def weigh_paired(t, a, b, weight):
             nc.scalar.activation(out=pairs[:, t // 2, a - DIRECT : b - DIRECT, t % 2], in_=window[t][:, a:b], func=COPY, scale=weight)
@@ -149,22 +151,37 @@ def tile_picked_blkmix_gelu_po_kernel(
         for n, (t, a, b, tag) in enumerate(early):
             scatter(t, a, b, project(n, t, a, b, tag))
         quantise_wa(2)
+        held = {tag: weight_copy(2, tag) for tag in ("direct", "paired")}
         activated = [project(len(early) + n, t, a, b, tag) for n, (t, a, b, tag) in enumerate(late)]
         for (t, a, b, tag), g in zip(late, activated):
             scatter(t, a, b, g)
             if b == H and t < LANES - 1:
                 weight = gt_sb[:, t : t + 1]
-                weigh_direct(t, weight_copy(t, "direct") if t == 2 else weight)
-                weigh_paired(t, DIRECT, DEAL_AFTER, weight_copy(t, "paired") if t == 2 else weight)
-                weigh_paired(t, DEAL_AFTER, U, weight)
-        w1s = tile([P, N], U8, "w1s", "wa_raw2")
-        deal(nc.gpsimd, w1s[:], w1s_raw[:])
+                if t < 2:
+                    weigh_direct(t, 0, DIRECT, weight)
+                    weigh_paired(t, DIRECT, PAIRED_END, weight)
+                    nc.gpsimd.tensor_scalar(
+                        out=z_bf[:, PAIRED_END:U, t],
+                        in0=window[t][:, PAIRED_END:U],
+                        scalar1=weight,
+                        scalar2=0.0,
+                        op0=MULT,
+                        op1=ADD,
+                    )
+                else:
+                    weigh_direct(t, 0, DIRECT, held["direct"])
+                    weigh_direct(t, PAIRED_END, U, weight)
+                    weigh_paired(t, DIRECT, DEAL_AFTER, held["paired"])
+                    weigh_paired(t, DEAL_AFTER, PAIRED_END, weight)
+        w1w = tile([P, N], U32, "w1w", "wa_raw2")
+        deal(nc.gpsimd, w1w[:], w1_raw[:].bitcast(U32))
 
         z_w = tile([P, U], U32, "z_w")
         z_s = tile([P, U], U8, "z_s")
-        last_weight = weight_copy(LANES - 1, "direct")
-        w1w = tile([P, N], U32, "w1w", "paired")
-        deal(nc.gpsimd, w1w[:], w1_raw[:].bitcast(U32))
+        last_weight = tile([P, 1], F32, "last_weight", "direct")
+        nc.vector.tensor_copy(out=last_weight[:], in_=gt_sb[:, LANES - 1 : LANES])
+        w1s = tile([P, N], U8, "w1s", "paired")
+        deal(nc.gpsimd, w1s[:], w1s_raw[:])
 
         def weave(a, b):
             nc.vector.tensor_copy(
@@ -175,13 +192,14 @@ def tile_picked_blkmix_gelu_po_kernel(
         def quantise_z(a, b):
             quantise(z_w[:, a:b], z_s[:, a:b], z_bf[:, a:b, :])
 
-        for a in range(DIRECT, U, 256):
+        for a in range(DIRECT, PAIRED_END, 256):
             weigh_paired(LANES - 1, a, a + 256, gt_sb[:, LANES - 1 : LANES])
+        weigh_direct(LANES - 1, PAIRED_END, U, gt_sb[:, LANES - 1 : LANES])
         for a in (0, 128):
             nc.vector.tensor_scalar(
                 out=z_bf[:, a : a + 128, LANES - 1],
                 in0=window[LANES - 1][:, a : a + 128],
-                scalar1=last_weight,
+                scalar1=last_weight[:],
                 scalar2=None,
                 op0=MULT,
             )
@@ -190,9 +208,7 @@ def tile_picked_blkmix_gelu_po_kernel(
         weave(256, 512)
         weave(512, 768)
         quantise_z(256, 512)
-        weave(768, U)
-        quantise_z(512, 768)
-        quantise_z(768, U)
+        quantise_z(512, U)
 
         out_rows = out_0.rearrange("(p t) n -> p t n", t=LANES)
         out_words = out_1[0].rearrange("p n t -> p (n t)").bitcast(I32)

@@ -49,7 +49,7 @@ def tile_picked_blkmix_gelu_po_kernel(
         ps = ctx.enter_context(tc.psum_pool(name="ps", bufs=1))
 
         def tile(shape, dtype, name, tag=None):
-            return sb.tile(shape, dtype, name=name, tag=tag or name, align_bytes=64)
+            return sb.tile(shape, dtype, name=name, tag=tag or name, align_bytes=256)
 
         def product(out, lhs_words, lhs_scales, rhs_words, rhs_scales):
             nc.tensor.matmul_mx(

@@ -212,7 +212,12 @@ def tile_picked_blkmix_gelu_po_kernel(
 
         out_rows = out_0.rearrange("(p t) n -> p t n", t=LANES)
         out_words = out_1[0].rearrange("p n t -> p (n t)").bitcast(I32)
-        result = tile([P, LANES, U], F32, "result")
+        blocks = {a: tile([P, LANES, b - a], F32, "result%d" % a) for a, b in ((0, 256), (256, 512), (512, U))}
+
+        def result(lo, hi, a, b):
+            start = max(s for s in blocks if s <= a)
+            return blocks[start][:, lo:hi, a - start : b - start]
+
         o_bf = tile([P, U, LANES], BF16, "o_bf")
         o_w = tile([P, U], I32, "o_w")
         o_s = tile([P, U], U8, "o_s")
@@ -225,16 +230,13 @@ def tile_picked_blkmix_gelu_po_kernel(
             product(acc[bank][:, a - start : b - start], w1w[:, rows], w1s[:, rows], z_w[:, a:b], z_s[:, a:b])
 
         def empty(copy, bank, t, a, b):
-            copy(out=result[:, t, a:b], in_=acc[bank][:, 0 : b - a])
+            copy(out=result(t, t + 1, a, b)[:, 0, :], in_=acc[bank][:, 0 : b - a])
 
         def store(lo, hi, a, b):
-            nc.sync.dma_start(out=out_rows[:, lo:hi, a:b], in_=result[:, lo:hi, a:b])
-
-        def round_early(a, b):
-            nc.vector.tensor_copy(out=o_bf[:, a:b, :], in_=result[:, :, a:b].rearrange("p t c -> p c t"))
+            nc.sync.dma_start(out=out_rows[:, lo:hi, a:b], in_=result(lo, hi, a, b))
 
         def round_late(copy, a, b):
-            interleave(copy, o_bf[:, a:b, :], result[:, :, a:b])
+            interleave(copy, o_bf[:, a:b, :], result(0, LANES, a, b))
 
         def quantise_out(a, b):
             quantise(o_w[:, a:b], o_s[:, a:b], o_bf[:, a:b, :])
@@ -254,8 +256,8 @@ def tile_picked_blkmix_gelu_po_kernel(
             empty(on_scalar if t % 2 else on_vector, 4 + t, t, 256, 512)
             if t % 2:
                 store(t - 1, t + 1, 256, 512)
-        round_early(0, 256)
-        round_early(256, 512)
+        round_late(on_vector, 0, 256)
+        round_late(on_vector, 256, 512)
         for t, copy in ((0, on_scalar), (1, on_scalar), (3, on_vector), (2, on_scalar)):
             mix(t, t, 512, U, 512)
             empty(copy, t, t, 512, U)

@@ -23,7 +23,7 @@ BANK = 512
 WA_PIECES = ((0, 128), (128, 256), (256, 512))
 DIRECT = 256
 PAIRED_END = 768
-DEAL_AFTER = 384
+THIN = 32
 SCALAR_ROUNDS_FROM = 832
 
 
@@ -151,7 +151,7 @@ def tile_picked_blkmix_gelu_po_kernel(
         for n, (t, a, b, tag) in enumerate(early):
             scatter(t, a, b, project(n, t, a, b, tag))
         quantise_wa(2)
-        held = {tag: weight_copy(2, tag) for tag in ("direct", "paired")}
+        held = {tag: weight_copy(2, tag) for tag in ("direct",)}
         activated = [project(len(early) + n, t, a, b, tag) for n, (t, a, b, tag) in enumerate(late)]
         for (t, a, b, tag), g in zip(late, activated):
             scatter(t, a, b, g)
@@ -171,17 +171,16 @@ def tile_picked_blkmix_gelu_po_kernel(
                 else:
                     weigh_direct(t, 0, DIRECT, held["direct"])
                     weigh_direct(t, PAIRED_END, U, weight)
-                    weigh_paired(t, DIRECT, DEAL_AFTER, held["paired"])
-                    weigh_paired(t, DEAL_AFTER, PAIRED_END, weight)
-        w1w = tile([P, N], U32, "w1w", "wa_raw2")
-        deal(nc.gpsimd, w1w[:], w1_raw[:].bitcast(U32))
+                    weigh_paired(t, DIRECT, PAIRED_END, weight)
+        w1s = tile([P, N], U8, "w1s", "wa_raw2")
+        deal(nc.gpsimd, w1s[:], w1s_raw[:])
 
         z_w = tile([P, U], U32, "z_w")
         z_s = tile([P, U], U8, "z_s")
         last_weight = tile([P, 1], F32, "last_weight", "direct")
         nc.vector.tensor_copy(out=last_weight[:], in_=gt_sb[:, LANES - 1 : LANES])
-        w1s = tile([P, N], U8, "w1s", "paired")
-        deal(nc.gpsimd, w1s[:], w1s_raw[:])
+        w1w = tile([P, N], U32, "w1w", "g6")
+        deal(nc.gpsimd, w1w[:], w1_raw[:].bitcast(U32))
 
         def weave(a, b):
             nc.vector.tensor_copy(
@@ -243,8 +242,9 @@ def tile_picked_blkmix_gelu_po_kernel(
             nc.sync.dma_start(out=out_words[:, a:b], in_=o_w[:, a:b])
 
         on_scalar, on_vector = nc.scalar.copy, nc.vector.tensor_copy
-        unread = ps.tile([P, BANK], F32, name="unread", tag="bank7")
-        product(unread[:], w1w[:, 0:P], w1s[:, 0:P], wa_w[:], wa_s[:])
+        unread = ps.tile([THIN, BANK], F32, name="unread", tag="bank7")
+        for n in range(4):
+            product(unread[:], w1w[:, 0:THIN], w1s[:, 0:THIN], wa_w[:], wa_s[:])
         for t in (0, 1):
             mix(t, t, 0, 128, 0)
         for t in range(LANES):

@@ -22,7 +22,7 @@ LANES = 4
 BANK = 512
 WA_PIECES = ((0, 128), (128, 256), (256, 512))
 DIRECT = 256
-PAIRED_END = 768
+PAIRED_END = 896
 THIN = 32
 SCALAR_ROUNDS_FROM = 832
 
@@ -191,8 +191,9 @@ def tile_picked_blkmix_gelu_po_kernel(
         def quantise_z(a, b):
             quantise(z_w[:, a:b], z_s[:, a:b], z_bf[:, a:b, :])
 
-        for a in range(DIRECT, PAIRED_END, 256):
-            weigh_paired(LANES - 1, a, a + 256, gt_sb[:, LANES - 1 : LANES])
+        woven = ((DIRECT, 512), (512, 768), (768, PAIRED_END))
+        for a, b in woven:
+            weigh_paired(LANES - 1, a, b, gt_sb[:, LANES - 1 : LANES])
         weigh_direct(LANES - 1, PAIRED_END, U, gt_sb[:, LANES - 1 : LANES])
         for a in (0, 128):
             nc.vector.tensor_scalar(
@@ -204,10 +205,12 @@ def tile_picked_blkmix_gelu_po_kernel(
             )
         quantise_z(0, 128)
         quantise_z(128, 256)
-        weave(256, 512)
-        weave(512, 768)
+        weave(*woven[0])
+        weave(*woven[1])
         quantise_z(256, 512)
-        quantise_z(512, U)
+        weave(*woven[2])
+        quantise_z(512, 768)
+        quantise_z(768, U)
 
         out_rows = out_0.rearrange("(p t) n -> p t n", t=LANES)
         out_words = out_1[0].rearrange("p n t -> p (n t)").bitcast(I32)
@@ -245,22 +248,37 @@ def tile_picked_blkmix_gelu_po_kernel(
         unread = ps.tile([THIN, BANK], F32, name="unread", tag="bank7")
         for n in range(4):
             product(unread[:], w1w[:, 0:THIN], w1s[:, 0:THIN], wa_w[:], wa_s[:])
-        for t in (0, 1):
-            mix(t, t, 0, 128, 0)
-        for t in range(LANES):
-            mix(t, t, 128 if t < 2 else 0, 256, 0)
+
+        def two_lanes(bank, lo, a):
+            both = ps.tile([P, 2, 128], F32, name="both", tag="bank%d" % bank)
+            for t in (lo, lo + 1):
+                rows = slice(P * t, P * (t + 1))
+                product(both[:, t - lo, :], w1w[:, rows], w1s[:, rows], z_w[:, a : a + 128], z_s[:, a : a + 128])
+            on_scalar(out=result(lo, lo + 2, a, a + 128), in_=both[:])
+            store(lo, lo + 2, a, a + 128)
+
+        two_lanes(0, 0, 0)
+        for t in (2, 3):
+            mix(t, t, 0, 256, 0)
             empty(on_scalar, t, t, 0, 256)
             store(t, t + 1, 0, 256)
+        two_lanes(1, 0, 128)
         for t in range(LANES):
             mix(4 + t, t, 256, 512, 256)
             empty(on_scalar if t % 2 else on_vector, 4 + t, t, 256, 512)
             if t % 2:
                 store(t - 1, t + 1, 256, 512)
+        for bank, t in ((0, 0), (3, 1), (1, 3)):
+            mix(bank, t, 512, 768, 512)
+        empty(on_scalar, 0, 0, 512, 768)
+        mix(2, 0, 768, U, 768)
+        empty(on_scalar, 2, 0, 768, U)
+        store(0, 1, 512, U)
         round_late(on_vector, 0, 256)
         round_late(on_vector, 256, 512)
-        for t, copy in ((0, on_scalar), (1, on_scalar), (3, on_vector), (2, on_scalar)):
-            mix(t, t, 512, U, 512)
-            empty(copy, t, t, 512, U)
+        for bank, t, a, copy in ((3, 1, 768, on_scalar), (1, 3, 768, on_vector), (5, 2, 512, on_scalar)):
+            mix(bank, t, a, U, 512)
+            empty(copy, bank, t, 512, U)
             if t < 2:
                 store(t, t + 1, 512, U)
         store(2, LANES, 512, U)

@@ -24,7 +24,7 @@ WA_PIECES = ((0, 128), (128, 256), (256, 512))
 DIRECT = 256
 PAIRED_END = 896
 THIN = 32
-SCALAR_ROUNDS_FROM = 832
+SCALAR_ROUNDS_FROM = 768
 
 
 def load_scale_rows(queue, plane, rows):
@@ -220,8 +220,8 @@ def tile_picked_blkmix_gelu_po_kernel(
             start = max(s for s in blocks if s <= a)
             return blocks[start][:, lo:hi, a - start : b - start]
 
-        o_bf = tile([P, U, LANES], BF16, "o_bf")
-        o_w = tile([P, U], I32, "o_w")
+        o_bf = {a: tile([P, b - a, LANES], BF16, "o_bf%d" % a, tag) for a, b, tag in ((0, 256, None), (256, 512, "z_w"), (512, U, None))}
+        o_w = tile([P, U], I32, "o_w", "g6")
         o_s = tile([P, U], U8, "o_s")
         acc = {}
 
@@ -237,55 +237,50 @@ def tile_picked_blkmix_gelu_po_kernel(
         def store(lo, hi, a, b):
             nc.sync.dma_start(out=out_rows[:, lo:hi, a:b], in_=result(lo, hi, a, b))
 
+        def packed(a, b):
+            start = max(s for s in o_bf if s <= a)
+            return o_bf[start][:, a - start : b - start, :]
+
         def round_late(copy, a, b):
-            interleave(copy, o_bf[:, a:b, :], result(0, LANES, a, b))
+            interleave(copy, packed(a, b), result(0, LANES, a, b))
 
         def quantise_out(a, b):
-            quantise(o_w[:, a:b], o_s[:, a:b], o_bf[:, a:b, :])
+            for lo in range(a, b, 256):
+                quantise(o_w[:, lo : lo + 256], o_s[:, lo : lo + 256], packed(lo, lo + 256))
             nc.sync.dma_start(out=out_words[:, a:b], in_=o_w[:, a:b])
 
         on_scalar, on_vector = nc.scalar.copy, nc.vector.tensor_copy
         unread = ps.tile([THIN, BANK], F32, name="unread", tag="bank7")
         for n in range(4):
             product(unread[:], w1w[:, 0:THIN], w1s[:, 0:THIN], wa_w[:], wa_s[:])
-
-        def two_lanes(bank, lo, a):
-            both = ps.tile([P, 2, 128], F32, name="both", tag="bank%d" % bank)
-            for t in (lo, lo + 1):
-                rows = slice(P * t, P * (t + 1))
-                product(both[:, t - lo, :], w1w[:, rows], w1s[:, rows], z_w[:, a : a + 128], z_s[:, a : a + 128])
-            on_scalar(out=result(lo, lo + 2, a, a + 128), in_=both[:])
-            store(lo, lo + 2, a, a + 128)
-
-        two_lanes(0, 0, 0)
-        for t in (2, 3):
-            mix(t, t, 0, 256, 0)
+        for t in (0, 1):
+            mix(t, t, 0, 128, 0)
+        for t in range(LANES):
+            mix(t, t, 128 if t < 2 else 0, 256, 0)
             empty(on_scalar, t, t, 0, 256)
             store(t, t + 1, 0, 256)
-        two_lanes(1, 0, 128)
         for t in range(LANES):
             mix(4 + t, t, 256, 512, 256)
             empty(on_scalar if t % 2 else on_vector, 4 + t, t, 256, 512)
             if t % 2:
                 store(t - 1, t + 1, 256, 512)
-        for bank, t in ((0, 0), (3, 1), (1, 3)):
+        for bank, t in ((0, 0), (2, 1), (3, 3)):
             mix(bank, t, 512, 768, 512)
         empty(on_scalar, 0, 0, 512, 768)
-        mix(2, 0, 768, U, 768)
-        empty(on_scalar, 2, 0, 768, U)
+        mix(1, 0, 768, U, 768)
+        empty(on_scalar, 1, 0, 768, U)
         store(0, 1, 512, U)
         round_late(on_vector, 0, 256)
-        round_late(on_vector, 256, 512)
-        for bank, t, a, copy in ((3, 1, 768, on_scalar), (1, 3, 768, on_vector), (5, 2, 512, on_scalar)):
+        for bank, t, a, copy in ((2, 1, 768, on_scalar), (3, 3, 768, on_vector), (5, 2, 512, on_scalar)):
             mix(bank, t, a, U, 512)
             empty(copy, bank, t, 512, U)
             if t < 2:
                 store(t, t + 1, 512, U)
         store(2, LANES, 512, U)
+        round_late(on_vector, 256, 512)
         quantise_out(0, 512)
         round_late(on_scalar, SCALAR_ROUNDS_FROM, U)
         round_late(on_vector, 512, 768)
-        round_late(on_vector, 768, SCALAR_ROUNDS_FROM)
         quantise_out(512, 768)
         quantise_out(768, U)
         for r in range(4):

@@ -124,7 +124,9 @@ def tile_picked_blkmix_gelu_po_kernel(
         def project(n, t, a, b, tag):
             y = ps.tile([P, b - a], F32, name="y", tag="bank%d" % n)
             tokens = slice(P * t, P * (t + 1))
-            product(y[:], xw[:, tokens], xs[:, tokens], wa_w[:, a:b], wa_s[:, a:b])
+            cuts = (a, 256, b) if b - a == 384 else (a, b)
+            for lo, hi in zip(cuts, cuts[1:]):
+                product(y[:, lo - a : hi - a], xw[:, tokens], xs[:, tokens], wa_w[:, lo:hi], wa_s[:, lo:hi])
             g = tile([P, b - a], F32, "g%d" % n, tag)
             nc.scalar.activation(out=g[:], in_=y[:], func=GELU)
             return g
@@ -146,8 +148,8 @@ def tile_picked_blkmix_gelu_po_kernel(
             nc.gpsimd.tensor_copy(out=weight[:], in_=gt_sb[:, t : t + 1])
             return weight[:]
 
-        early = ((0, 0, 128, "wa_raw1"), (1, 0, 256, None), (0, 128, 256, None))
-        late = ((2, 0, 256, "wa_raw2"), (0, 256, H, None), (1, 256, H, None), (2, 256, H, None), (3, 0, H, None))
+        early = ((0, 0, 128, "wa_raw1"), (1, 0, 256, None))
+        late = ((2, 0, 256, "wa_raw2"), (0, 128, H, None), (1, 256, H, None), (2, 256, H, None), (3, 0, H, None))
         for n, (t, a, b, tag) in enumerate(early):
             scatter(t, a, b, project(n, t, a, b, tag))
         quantise_wa(2)
@@ -179,7 +181,7 @@ def tile_picked_blkmix_gelu_po_kernel(
         z_s = tile([P, U], U8, "z_s")
         last_weight = tile([P, 1], F32, "last_weight", "direct")
         nc.vector.tensor_copy(out=last_weight[:], in_=gt_sb[:, LANES - 1 : LANES])
-        w1w = tile([P, N], U32, "w1w", "g6")
+        w1w = tile([P, N], U32, "w1w", "g5")
         deal(nc.gpsimd, w1w[:], w1_raw[:].bitcast(U32))
 
         def weave(a, b):
@@ -221,7 +223,7 @@ def tile_picked_blkmix_gelu_po_kernel(
             return blocks[start][:, lo:hi, a - start : b - start]
 
         o_bf = {a: tile([P, b - a, LANES], BF16, "o_bf%d" % a, tag) for a, b, tag in ((0, 256, None), (256, 512, "z_w"), (512, U, None))}
-        o_w = tile([P, U], I32, "o_w", "g6")
+        o_w = tile([P, U], I32, "o_w", "g5")
         o_s = tile([P, U], U8, "o_s")
         acc = {}
 

from contextlib import ExitStack

import concourse.mybir as mybir

K, T, S, H, U, N = 512, 2048, 512, 512, 1024, 512
FLOPS = 2 * K * S * H + 2 * S * N * U

F32 = mybir.dt.float32
BF16 = mybir.dt.bfloat16
I32 = mybir.dt.int32
U32 = mybir.dt.uint32
U16 = mybir.dt.uint16
U8 = mybir.dt.uint8
FP8X4 = mybir.dt.float8_e4m3fn_x4
GELU = mybir.ActivationFunctionType.Gelu_apprx_tanh
COPY = mybir.ActivationFunctionType.Copy
MULT = mybir.AluOpType.mult
ADD = mybir.AluOpType.add

P = 128
LANES = 4
BANK = 512
WA_PIECES = ((0, 128), (128, 256), (256, 512))
DIRECT = 256
PAIRED_END = 896
THIN = 32
SCALAR_ROUNDS_FROM = 768


def load_scale_rows(queue, plane, rows):
    for r in range(4):
        queue.dma_start(out=plane[r:P:32, :].bitcast(I32), in_=rows[r:16:4, :].bitcast(I32))


def deal(engine, dealt, plain):
    engine.tensor_copy(out=dealt.rearrange("p (t m) -> p t m", t=LANES), in_=plain.rearrange("p (m t) -> p t m", t=LANES))


def interleave(copy, packed, rows):
    copy(out=packed.rearrange("p (c i) t -> p c t i", i=4), in_=rows.rearrange("p t (c i) -> p c t i", i=4))


def tile_picked_blkmix_gelu_po_kernel(
    tc, x_words, x_scales, wa, gt, w1_words, w1_scales, offs, fl, out_0, out_1, out_2
):
    nc = tc.nc
    with ExitStack() as ctx:
        sb = ctx.enter_context(tc.tile_pool(name="sb", bufs=1))
        ps = ctx.enter_context(tc.psum_pool(name="ps", bufs=1))

        def tile(shape, dtype, name, tag=None):
            return sb.tile(shape, dtype, name=name, tag=tag or name, align_bytes=256)

        def product(out, lhs_words, lhs_scales, rhs_words, rhs_scales):
            nc.tensor.matmul_mx(
                out=out,
                lhsT=lhs_words.bitcast(FP8X4),
                lhsT_scale=lhs_scales,
                rhs=rhs_words.bitcast(FP8X4),
                rhs_scale=rhs_scales,
                start=True,
                stop=True,
            )

        def quantise(words, scales, packed):
            nc.vector.quantize_mx(out=words.bitcast(FP8X4), scales=scales, in_=packed.rearrange("p c t -> p (c t)"))

        offs_sb = tile([P, S // 16], U16, "offs_sb")
        fl_sb = tile([P, H // 16], U16, "fl_sb")
        x_table = tile([P, T], I32, "x_table")
        xs_table = tile([P, T], U8, "xs_table")
        w1_raw = tile([P, N], I32, "w1_raw")
        w1s_raw = tile([P, N], U8, "w1s_raw")
        gt_sb = tile([P, LANES], F32, "gt_sb")
        wa_raw = [tile([P, LANES, b - a], F32, "wa_raw%d" % n) for n, (a, b) in enumerate(WA_PIECES)]
        wa_rows = wa.rearrange("(p j) c -> p j c", j=LANES)
        window = {}

        def clear_window(engine, t, tag):
            window[t] = tile([P, U], F32, "window%d" % t, tag)
            engine.memset(window[t][:], 0.0)

        def load_wa(n):
            a, b = WA_PIECES[n]
            nc.sync.dma_start(out=wa_raw[n][:], in_=wa_rows[:, :, a:b])

        nc.gpsimd.memset(xs_table[:].bitcast(I32), 0)
        clear_window(nc.vector, 0, None)
        warmed = tile([P, 1], F32, "warmed")
        nc.scalar.activation(out=warmed[:], in_=window[0][:, 0:1], func=GELU)
        clear_window(nc.vector, 1, None)
        load_wa(0)
        nc.sync.dma_start(offs_sb[:], offs)
        load_scale_rows(nc.sync, xs_table, x_scales[0])
        nc.sync.dma_start(out=x_table[:], in_=x_words[0].rearrange("p n t -> p (n t)").bitcast(I32))
        load_wa(1)
        nc.sync.dma_start(fl_sb[:], fl)
        load_wa(2)
        nc.sync.dma_start(out=w1_raw[:], in_=w1_words[0].rearrange("p n t -> p (n t)").bitcast(I32))
        nc.sync.dma_start(out=gt_sb[:], in_=gt.rearrange("(p t) o -> p (t o)", t=LANES))
        nc.gpsimd.memset(w1s_raw[:].bitcast(I32), 0)
        load_scale_rows(nc.sync, w1s_raw, w1_scales[0])

        xs_picked = tile([P, S], U8, "xs_picked")
        xs = tile([P, S], U8, "xs")
        xw = tile([P, S], U32, "xw")
        wa_w = tile([P, H], U32, "wa_w")
        wa_s = tile([P, H], U8, "wa_s")

        def quantise_wa(n):
            a, b = WA_PIECES[n]
            rounded = tile([P, b - a, LANES], BF16, "wa_bf%d" % n)
            interleave(nc.scalar.copy, rounded[:], wa_raw[n][:])
            quantise(wa_w[:, a:b], wa_s[:, a:b], rounded[:])

        nc.vector.tensor_copy(out=xs_picked[:], in_=xs_table[:].indirect(offs_sb[:]))
        deal(nc.vector, xs[:], xs_picked[:])
        quantise_wa(0)
        nc.vector.tensor_copy(out=xw[:].rearrange("p (t m) -> p m t", t=LANES), in_=x_table[:].bitcast(U32).indirect(offs_sb[:]))
        quantise_wa(1)
        clear_window(nc.gpsimd, 3, "wa_bf0")
        clear_window(nc.gpsimd, 2, "wa_bf1")

        def project(n, t, a, b, tag):
            y = ps.tile([P, b - a], F32, name="y", tag="bank%d" % n)
            tokens = slice(P * t, P * (t + 1))
            cuts = (a, 256, b) if b - a == 384 else (a, b)
            for lo, hi in zip(cuts, cuts[1:]):
                product(y[:, lo - a : hi - a], xw[:, tokens], xs[:, tokens], wa_w[:, lo:hi], wa_s[:, lo:hi])
            g = tile([P, b - a], F32, "g%d" % n, tag)
            nc.scalar.activation(out=g[:], in_=y[:], func=GELU)
            return g

        def scatter(t, a, b, g):
            nc.vector.tensor_copy(out=window[t][:].indirect(fl_sb[:, a // 16 : b // 16]), in_=g[:])

        z_bf = tile([P, U, LANES], BF16, "z_bf")
        pairs = tile([P, 2, PAIRED_END - DIRECT, 2], BF16, "pairs")

        def weigh_direct(t, a, b, weight):
            nc.scalar.activation(out=z_bf[:, a:b, t], in_=window[t][:, a:b], func=COPY, scale=weight)

        def weigh_paired(t, a, b, weight):
            nc.scalar.activation(out=pairs[:, t // 2, a - DIRECT : b - DIRECT, t % 2], in_=window[t][:, a:b], func=COPY, scale=weight)

        def weight_copy(t, tag):
            weight = tile([P, 1], F32, tag + "%d" % t, tag)
            nc.gpsimd.tensor_copy(out=weight[:], in_=gt_sb[:, t : t + 1])
            return weight[:]

        early = ((0, 0, 128, "wa_raw1"), (1, 0, 256, None))
        late = ((2, 0, 256, "wa_raw2"), (0, 128, H, None), (1, 256, H, None), (2, 256, H, None), (3, 0, H, None))
        for n, (t, a, b, tag) in enumerate(early):
            scatter(t, a, b, project(n, t, a, b, tag))
        quantise_wa(2)
        held = {tag: weight_copy(2, tag) for tag in ("direct",)}
        activated = [project(len(early) + n, t, a, b, tag) for n, (t, a, b, tag) in enumerate(late)]
        for (t, a, b, tag), g in zip(late, activated):
            scatter(t, a, b, g)
            if b == H and t < LANES - 1:
                weight = gt_sb[:, t : t + 1]
                if t < 2:
                    weigh_direct(t, 0, DIRECT, weight)
                    weigh_paired(t, DIRECT, PAIRED_END, weight)
                    nc.gpsimd.tensor_scalar(
                        out=z_bf[:, PAIRED_END:U, t],
                        in0=window[t][:, PAIRED_END:U],
                        scalar1=weight,
                        scalar2=0.0,
                        op0=MULT,
                        op1=ADD,
                    )
                else:
                    weigh_direct(t, 0, DIRECT, held["direct"])
                    weigh_direct(t, PAIRED_END, U, weight)
                    weigh_paired(t, DIRECT, PAIRED_END, weight)
        w1s = tile([P, N], U8, "w1s", "wa_raw2")
        deal(nc.gpsimd, w1s[:], w1s_raw[:])

        z_w = tile([P, U], U32, "z_w")
        z_s = tile([P, U], U8, "z_s")
        last_weight = tile([P, 1], F32, "last_weight", "direct")
        nc.vector.tensor_copy(out=last_weight[:], in_=gt_sb[:, LANES - 1 : LANES])
        w1w = tile([P, N], U32, "w1w", "g5")
        deal(nc.gpsimd, w1w[:], w1_raw[:].bitcast(U32))

        def weave(a, b):
            nc.vector.tensor_copy(
                out=z_bf[:, a:b, :].rearrange("p c (h e) -> p c h e", h=2),
                in_=pairs[:, :, a - DIRECT : b - DIRECT, :].rearrange("p h c e -> p c h e"),
            )

        def quantise_z(a, b):
            quantise(z_w[:, a:b], z_s[:, a:b], z_bf[:, a:b, :])

        woven = ((DIRECT, 512), (512, 768), (768, PAIRED_END))
        for a, b in woven:
            weigh_paired(LANES - 1, a, b, gt_sb[:, LANES - 1 : LANES])
        weigh_direct(LANES - 1, PAIRED_END, U, gt_sb[:, LANES - 1 : LANES])
        for a in (0, 128):
            nc.vector.tensor_scalar(
                out=z_bf[:, a : a + 128, LANES - 1],
                in0=window[LANES - 1][:, a : a + 128],
                scalar1=last_weight[:],
                scalar2=None,
                op0=MULT,
            )
        quantise_z(0, 128)
        quantise_z(128, 256)
        weave(*woven[0])
        weave(*woven[1])
        quantise_z(256, 512)
        weave(*woven[2])
        quantise_z(512, 768)
        quantise_z(768, U)

        out_rows = out_0.rearrange("(p t) n -> p t n", t=LANES)
        out_words = out_1[0].rearrange("p n t -> p (n t)").bitcast(I32)
        blocks = {a: tile([P, LANES, b - a], F32, "result%d" % a) for a, b in ((0, 256), (256, 512), (512, U))}

        def result(lo, hi, a, b):
            start = max(s for s in blocks if s <= a)
            return blocks[start][:, lo:hi, a - start : b - start]

        o_bf = {a: tile([P, b - a, LANES], BF16, "o_bf%d" % a, tag) for a, b, tag in ((0, 256, None), (256, 512, "z_w"), (512, U, None))}
        o_w = tile([P, U], I32, "o_w", "g5")
        o_s = tile([P, U], U8, "o_s")
        acc = {}

        def mix(bank, t, a, b, start):
            if a == start:
                acc[bank] = ps.tile([P, BANK], F32, name="acc", tag="bank%d" % bank)
            rows = slice(P * t, P * (t + 1))
            product(acc[bank][:, a - start : b - start], w1w[:, rows], w1s[:, rows], z_w[:, a:b], z_s[:, a:b])

        def empty(copy, bank, t, a, b):
            copy(out=result(t, t + 1, a, b)[:, 0, :], in_=acc[bank][:, 0 : b - a])

        def store(lo, hi, a, b):
            nc.sync.dma_start(out=out_rows[:, lo:hi, a:b], in_=result(lo, hi, a, b))

        def packed(a, b):
            start = max(s for s in o_bf if s <= a)
            return o_bf[start][:, a - start : b - start, :]

        def round_late(copy, a, b):
            interleave(copy, packed(a, b), result(0, LANES, a, b))

        def quantise_out(a, b):
            for lo in range(a, b, 256):
                quantise(o_w[:, lo : lo + 256], o_s[:, lo : lo + 256], packed(lo, lo + 256))
            nc.sync.dma_start(out=out_words[:, a:b], in_=o_w[:, a:b])

        on_scalar, on_vector = nc.scalar.copy, nc.vector.tensor_copy
        unread = ps.tile([THIN, BANK], F32, name="unread", tag="bank7")
        for n in range(4):
            product(unread[:], w1w[:, 0:THIN], w1s[:, 0:THIN], wa_w[:], wa_s[:])
        for t in (0, 1):
            mix(t, t, 0, 128, 0)
        for t in range(LANES):
            mix(t, t, 128 if t < 2 else 0, 256, 0)
            empty(on_scalar, t, t, 0, 256)
            store(t, t + 1, 0, 256)
        for t in range(LANES):
            mix(4 + t, t, 256, 512, 256)
            empty(on_scalar if t % 2 else on_vector, 4 + t, t, 256, 512)
            if t % 2:
                store(t - 1, t + 1, 256, 512)
        for bank, t in ((0, 0), (2, 1), (3, 3)):
            mix(bank, t, 512, 768, 512)
        empty(on_scalar, 0, 0, 512, 768)
        mix(1, 0, 768, U, 768)
        empty(on_scalar, 1, 0, 768, U)
        store(0, 1, 512, U)
        round_late(on_vector, 0, 256)
        for bank, t, a, copy in ((2, 1, 768, on_scalar), (3, 3, 768, on_vector), (5, 2, 512, on_scalar)):
            mix(bank, t, a, U, 512)
            empty(copy, bank, t, 512, U)
            if t < 2:
                store(t, t + 1, 512, U)
        store(2, LANES, 512, U)
        round_late(on_vector, 256, 512)
        quantise_out(0, 512)
        round_late(on_scalar, SCALAR_ROUNDS_FROM, U)
        round_late(on_vector, 512, 768)
        quantise_out(512, 768)
        quantise_out(768, U)
        for r in range(4):
            queue = nc.scalar if r % 2 else nc.sync
            queue.dma_start(out=out_2[0, r:16:4, :].bitcast(I32), in_=o_s[r:P:32, :].bitcast(I32))
